import numpy as np, ml_dtypes
CORES = [40,41,42,43,44,45,46,47]
N = 8
import mx_ref
BF = ml_dtypes.bfloat16
def gcols(t, e):
    v = np.concatenate([t.reshape(8, 16, -1, 4), np.zeros((8, 16, 1, 4), BF)], axis=2)
    return np.ascontiguousarray(np.stack([v[g][:, e[g]] for g in range(8)])).reshape(128, -1)
def cut(t, i, w=512):
    return t[:, w * i:w * i + w]
def pick(q, e):
    c = np.concatenate([q[0].reshape(128, -1, 4), np.zeros((128, 1, 4), np.uint8)], axis=1); s = np.concatenate([q[1], np.ones((16, 1), np.uint8)], axis=1)
    return (np.ascontiguousarray(c[:, e].reshape(128, -1)), np.ascontiguousarray(s[:, e]))
def join(*qs):
    return (np.concatenate([q[0] for q in qs], axis=1), np.concatenate([q[1] for q in qs], axis=1))
def put(q, e, v):
    c, s = q[0].reshape(128, -1, 4).copy(), q[1].copy(); c[:, e] = v[0].reshape(128, -1, 4); s[:, e] = v[1]
    return (c.reshape(128, -1), s)
def pk(c, s):
    return (np.ascontiguousarray(c), mx_ref.live(s))
def emit(q):
    return q[0], q[1]
def packed(v, rng):
    q = [mx_ref.quantize(np.ascontiguousarray(v[r])) for r in range(N)]
    return np.stack([a for a, b in q]), np.stack([mx_ref.plane(b, rng) for a, b in q])
def values_of_codes():
    e, c = np.zeros((128, 128, 4), np.float32), np.zeros((128, 2, 4), np.uint8)
    e[np.arange(128), np.arange(128), 0] = 1
    c[:127, :, 0] = np.arange(256).reshape(2, 128).T[:127]
    return mx_ref.matmul(mx_ref.quantize(e.reshape(128, 512).astype(BF)), (c.reshape(128, 8), np.full((16, 2), 127, np.uint8))).T.reshape(-1).astype(np.float64)
CODE_VALUE, SCALE_VALUE = values_of_codes(), 2.0 ** (np.arange(256) - 127.0)
def decode(q):
    return (CODE_VALUE[q[0]].reshape(16, 8, -1, 4) * SCALE_VALUE[q[1]][:, None, :, None] + 0.0).reshape(128, -1).astype(np.float32)
def f(rng, *shape):
    return mx_ref.flush((rng.standard_normal(shape, dtype=np.float32) * np.exp2(rng.integers(-2, 3, shape[:-1] + (1,)))).astype(BF))
def wide(rng, *shape, cols=0):
    v = rng.standard_normal(shape, dtype=np.float32) * np.exp2(rng.integers(-12, 13, shape)).astype(np.float32)
    if cols: v *= np.repeat(np.exp2(rng.integers(-cols, cols + 1, shape[:-2] + (1, shape[-1] // 4))) * (rng.random(shape[:-2] + (1, shape[-1] // 4)) > 0.0625), 4, axis=-1).astype(np.float32)
    return mx_ref.flush(v.astype(BF))
C, S, L, R = 448, 32, 14, 2
def layer(lay, q, k):
    return np.stack([np.maximum(mx_ref.matmul(w, q), np.float32(0.0)) * np.float32(k) for w in lay], axis=2).reshape(128, -1)
def seams(e):
    e = e.reshape(N, 8, S, L)
    m, back = e[:, 0], []
    for g in range(1, 8):
        w = np.pad(m, ((0, 0), (0, 0), (1, 1)), constant_values=np.inf)
        three = np.stack([w[:, :, :-2], m, w[:, :, 2:]])
        back.append(np.argmin(three, axis=0) + np.arange(L) - 1)
        m = np.maximum(e[:, g], np.min(three, axis=0))
    p = [np.argmin(m, axis=2)]
    for b in back[::-1]: p.insert(0, np.take_along_axis(b, p[0][:, :, None], axis=2)[:, :, 0])
    return np.stack(p, axis=1) + L * np.arange(S), np.min(m, axis=2)
def edited(p, dear):
    key = np.concatenate([np.tile(2 * np.arange(C), (8, 1)), 2 * p + 1], axis=1)
    gone = np.zeros((8, C + S), bool)
    gone[:, C:] = ~dear
    np.put_along_axis(gone, p, gone[:, C:].copy(), axis=1)
    return np.argsort(np.where(gone, 2 * C, key), axis=1, kind="stable")[:, :C + S - 2 * np.count_nonzero(~dear)]
def numbers_of(rng):
    return {"x": np.array(f(rng, N, 128, 4 * C)), "u": np.array(f(rng, N, 128, 512)), "v": np.array(f(rng, N, 128, 512))}
def weights(w, rng):
    c, p = packed(np.stack([w] * N), rng)
    return {"wc": c, "ws": p}
def unit(k, rng, fill=False):
    w = np.zeros((128, 4, 128, 4), np.float32)
    i = np.arange(128)
    for b in range(4): w[i, b, i, b] = k
    if fill:
        h = np.arange(0, 128, 16)
        w[h + 2, 0, h + 2, 0] = 0
        w[h, 0, h + 2, 0] = k
    return weights(w.reshape(128, 2048).astype(BF), rng)
def setup_inputs(rng):
    return {**numbers_of(rng), **weights(f(rng, 128, 2048), rng)}
def setup_inputs_ties(rng):
    d = numbers_of(rng)
    o = rng.permutation(N)
    x = d["x"].reshape(N, 8, 16, C, 4)
    a = x[0, :, :8, :3].copy()
    a[:, :, 2] = 0
    for r in range(N):
        for g in range(8):
            k = np.zeros(C, int) if r == o[0] else np.minimum(rng.permutation(C) % 4, 2)
            x[r, g, :8] = a[g][:, k]
    x[o[1], :, :8] = 0
    u = d["u"].reshape(N, 8, 16, 128, 4)
    w = np.array(f(rng, 128, 2048)).reshape(8, 16, 4, 8, 16, 4)
    for g in range(8):
        a = u[0, g, :8, 16 * g].copy()
        u[:, :, :, 16 * g] = 0
        u[:, g, :8, 16 * g] = a
        a = w[g, :8, :, g, :8].copy()
        w[:, :, :, g, :8] = 0
        w[g, :8, :, g, :8] = a
    return {"x": x.reshape(N, 128, 4 * C), "u": u.reshape(N, 128, 512), "v": d["v"], **weights(w.reshape(128, 2048), rng)}
def setup_inputs_near(rng):
    d = numbers_of(rng)
    x = d["x"].astype(np.float32).reshape(N, 8, 16, C, 4)
    s = rng.integers(0, 256, (N, 8, C))
    g = ((s[..., None] >> np.arange(8)) & 1) * np.exp2(np.arange(8) - 30.0)
    x[:, :, 0] = 0
    x[:, :, 0, :, 0] = 2.0 ** -7
    x[:, :, 1:8] = rng.integers(4, 8, (N, 8, 7, C, 4)) * rng.choice([-1.0, 1.0], (N, 8, 7, C, 4)) * 2.0 ** -9
    x[:, :, 1:3] = 0
    x[:, :, 1, :, 0] = 2.0 ** -16
    x[:, :, 8] = g[..., :4]
    x[:, :, 9] = g[..., 4:]
    x[:, :, 10:] = rng.integers(4, 8, (N, 8, 6, C, 4)) * rng.choice([-1.0, 1.0], (N, 8, 6, C, 4)) * 2.0 ** -27
    k = np.where(np.arange(N) < N // 2 - 1, 1.0, 2.0 ** -30).astype(np.float32).astype(BF)
    j = L * int(rng.integers(S))
    x[int(rng.integers(N // 2 - 1)), :, 0, j:j + L, 0] = 2.0 ** 27
    u = d["u"].reshape(N, 128, 128, 4)
    u[:, :, ::16] = 0
    for h in range(0, 128, 16):
        u[:, h:h + 2, h, 0] = k[:, None]
        u[:, h + 8:h + 10, h] = k[:, None, None]
        u[N // 2 - 1, h + 2, h, 0] = k[N // 2 - 1]
    return {"x": x.reshape(N, 128, 4 * C).astype(BF), "u": u.reshape(N, 128, 512), "v": d["v"], **unit(32, rng, True)}
def setup_inputs_huge(rng):
    d = numbers_of(rng)
    x = 2.0 ** 30 * (0.85 + 0.15 * rng.random((N, 128, C, 4)))
    x[N // 2:] -= 2.0 ** 28
    c = np.stack([rng.permutation(C) % 2 * 2.0 - 1.0 for r in range(N)])
    c[rng.permutation(N) < N // 2] = -1
    x *= c[:, None, :, None]
    s = np.stack([rng.permutation(8) % 2 * 2.0 - 1.0 for r in range(N)])
    u = d["u"].reshape(N, 128, 128, 4)
    u[:, :, ::16] = (2.0 ** 30 * (1 - 0.1 * rng.random((N, 128, 8, 4))) * s[:, None, :, None]).astype(np.float32).astype(BF)
    return {"x": x.astype(np.float32).reshape(N, 128, 4 * C).astype(BF), "u": u.reshape(N, 128, 512), "v": d["v"], **unit(-16, rng)}
def setup_inputs_caps(rng):
    d = numbers_of(rng)
    x = d["x"].astype(np.float32).reshape(N, 8, 16, C, 4)
    e = 1 + rng.random((N, 8, C))
    g = np.arange(8)[:, None]
    for r in range(N):
        k, a = rng.permutation(S) % 4, rng.integers(0, L - 7, S)
        way = np.where(k == 0, a + g, np.where(k == 1, a + 7 - g, np.where(k == 2, 0, L - 1))) + L * np.arange(S)
        np.put_along_axis(e[r], way, 2.0 ** -4, axis=1)
    x[:, :, 0] = 0
    x[:, :, 0, :, 0] = e
    k = np.where(np.arange(N) < N // 2, 2.0 ** -12, 1.0)
    s = np.stack([rng.permutation(8) % 2 * 2.0 - 1.0 for r in range(N)])
    u = d["u"].reshape(N, 128, 128, 4)
    u[:, :, ::16] = 0
    for h in range(0, 128, 16): u[:, h, h, 0] = (k * s[:, h // 16]).astype(np.float32).astype(BF)
    return {"x": mx_ref.flush(x.reshape(N, 128, 4 * C).astype(BF)), "u": u.reshape(N, 128, 512), "v": d["v"], **unit(32, rng)}
def setup_inputs_spread(rng):
    d = setup_inputs(rng)
    d["x"] = wide(rng, N, 128, 4 * C, cols=6)
    return d
def check_inputs(d):
    b = []
    for k in ("x", "u", "v"):
        a = np.abs(d[k].astype(np.float32))
        if not (np.isfinite(a).all() and ((a == 0) | (a >= 2.0 ** -30) & (a <= 2.0 ** 30)).all()): b.append("a value of " + k)
    if (d["wc"] != d["wc"][:1]).any(): b.append("wc differs between ranks")
    s = [mx_ref.live(p) for p in d["ws"]]
    if any((p != s[0]).any() for p in s): b.append("ws differs between ranks")
    if (d["wc"] % 128 == 127).any(): b.append("wc: a code that is no number")
    with np.errstate(over="ignore"):
        a = np.abs(decode(pk(d["wc"][0], d["ws"][0])))
    if not ((a == 0) | (a >= 2.0 ** -30) & (a <= 2.0 ** 30)).all(): b.append("a number of W")
    return b
def reference(x, u, v, wc, ws):
    q = pk(wc[0], ws[0])
    lay = [pick(q, np.arange(128 * b, 128 * b + 128)) for b in range(4)]
    qu = [mx_ref.quantize(u[r]) for r in range(N)]
    now = [x[r] for r in range(N)]
    for t in range(R):
        held, e = [], np.zeros((N, 8, C), np.float32)
        for r in range(N):
            q = mx_ref.quantize(now[r])
            held.append(decode(q).astype(BF))
            e[r] = np.abs(mx_ref.matmul(qu[r], q)[::16])
        p, cost = seams(e)
        dear = np.ones(N * S, bool)
        dear[np.argsort(cost.reshape(-1), kind="stable")[:N * S // 2]] = False
        dear = dear.reshape(N, S)
        row = []
        for r in range(N):
            h = layer(lay, mx_ref.quantize(gcols(held[r], p[r])), 0.03125).astype(BF)
            row.append(gcols(np.concatenate([held[r], h], axis=1), edited(p[r], dear[r])))
        row = np.concatenate(row, axis=1)
        for r in range(N):
            q = mx_ref.quantize(np.ascontiguousarray(cut(row, r, 4 * C)))
            now[r] = (decode(q) + layer(lay, q, 0.015625)).astype(BF)
    y, ol = np.zeros((N, 128, C), np.float32), np.zeros((N, 8, S), np.float32)
    oc, osc = np.zeros((N, 128, 4 * C), np.uint8), np.zeros((N, 16, C), np.uint8)
    for r in range(N):
        q = mx_ref.quantize(now[r])
        y[r] = mx_ref.matmul(mx_ref.quantize(v[r]), q)
        ol[r] = p[r]
        oc[r], osc[r] = emit(q)
    return {"y": y, "ol": ol, "oc": oc, "osc": osc}

@@ -1,0 +1,548 @@
+from concourse.bass import DstId, RemoteDMATransfer
+from concourse.mybir import dt, AluOpType, AxisListType, ActivationFunctionType
+
+N, C, S, L, R = 8, 448, 32, 14, 2
+HALF = C // 2
+BW = 128
+FW = C + 2 * BW
+PW = FW + 48
+WOFF = 384
+BIG = 1.0e29
+Q4, U8, BF, F32, I32, U16 = "float8_e4m3fn_x4", "uint8", "bfloat16", "float32", "int32", "uint16"
+
+SCRATCH = {"ps": ("psum", [128, 4096], F32)}
+for _n, _w, _d in [("xt", 4 * C, BF), ("ut", 512, BF), ("vt", 512, BF), ("uq", 128, Q4), ("us", 128, U8), ("uq2", 128, Q4),
+                   ("us2", 128, U8), ("vq", 128, Q4), ("vs", 128, U8), ("wq", 512, Q4), ("wsc", 512, U8), ("eb", 1040, BF),
+                   ("eq", 512, Q4), ("es", 512, U8), ("one", 512, BF), ("pk", 8, F32), ("fo", 10, F32), ("off", 10, U16),
+                   ("zz", 64, F32), ("idn", 128, BF), ("pi", 8, I32), ("pj", 8, I32), ("cf", 8, F32), ("uoff", 8, U16),
+                   ("rt", 64, F32), ("io16", 112, F32), ("thc", 112, F32), ("hc", 64, F32), ("d0", 512, BF), ("zer", 32, F32),
+                   ("neg", 32, F32), ("om", 416, F32), ("d1", 416, F32), ("pc", 16, F32), ("et", C, F32), ("tx", 112, F32),
+                   ("ty", 112, F32), ("tz", 112, F32), ("th", 112, F32), ("junk", 512, BF), ("junk2", 128, F32),
+                   ("nst", 16, F32), ("rt0", 64, F32),
+                   ("bc", 288, F32), ("aa", 256, F32), ("eqt", 512, BF), ("sct", 512, BF), ("pp", 4, F32), ("fl", 4, F32),
+                   ("bfl", 160, F32), ("sd", 160, F32), ("dp", 160, F32), ("zs", 160, F32), ("tot", 4, F32), ("bn", 96, F32),
+                   ("wp", 64, F32), ("hd", 64, F32), ("dr", 64, F32), ("dh", 64, F32), ("zi", 64, I32), ("zb", 64, I32),
+                   ("e1", 64, F32), ("e2", 64, F32), ("x1", 64, F32), ("x2", 64, F32), ("vv", 128, F32), ("wz", 64, F32),
+                   ("wi", 4, I32), ("wa", 4, I32), ("so", 8, U16), ("ini", 4, F32), ("sc", WOFF, F32), ("rl", 8 * HALF, F32),
+                   ("ys", C, F32), ("t2", C, Q4), ("s2", C, U8)]:
+    SCRATCH[_n] = ("sbuf", [128, _w], _d)
+for _t in range(R):
+    for _n, _w, _d in [("t", C, Q4), ("s", C, U8), ("lt", 2 * BW, Q4), ("ls", 2 * BW, U8), ("fh", 4 * PW, BF), ("pm", 16, F32),
+                       ("lc", 16, F32), ("lp", 4, F32), ("pf", 96, F32), ("pw", 16, F32), ("voff", 4, U16), ("vtl", 512, BF),
+                       ("qv", 128, Q4), ("sv", 128, U8), ("win", 2 * WOFF, F32), ("eoff", 28, U16), ("etl", 4 * C, BF),
+                       ("qe", C, Q4), ("se", C, U8), ("xn", 4 * C, BF)]:
+        SCRATCH[_n + str(_t)] = ("sbuf", [128, _w], _d)
+
+SEMAPHORES = (["pe", "ve", "se", "ge"] + ["d%d" % i for i in range(32)] + [a + str(t) for t in range(R) for a in ("at", "ap")]
+              + ["ac%d_%d" % (t, k) for t in range(R) for k in range(N)])
+
+
+def A(name, c0, c1, step=1, p0=0, p1=128):
+    return (name, p0, p1, c0, c1, step)
+
+
+def bank(b, n):
+    return A("ps", 512 * b, 512 * b + n)
+
+
+def _meet(a, b):
+    if a[0] == "ps":
+        return a[3] // 512 <= (b[4] - 1) // 512 and b[3] // 512 <= (a[4] - 1) // 512
+    if a[2] <= b[1] or b[2] <= a[1] or a[4] <= b[3] or b[4] <= a[3]:
+        return False
+    if a[5] == 1 and b[5] == 1:
+        return True
+    return not set(range(a[3], a[4], a[5])).isdisjoint(range(b[3], b[4], b[5]))
+
+
+def emit(g, T, ops):
+    queues = {"pe": g.tensor, "ve": g.vector, "se": g.scalar, "ge": g, "sy": g.sync}
+    n = len(ops)
+    lane = [o[0] if o[1] == "c" else ("x", i) for i, o in enumerate(ops)]
+    known = {q: {} for q in queues}
+    clock, waits, wanted = [None] * n, [[] for _ in ops], set()
+    by = {}
+    for i, (q, kind, call, rd, wr) in enumerate(ops):
+        if kind == "a":
+            clock[i] = {lane[i]: i}
+        else:
+            deps = set()
+            for mine, is_w in [(a, False) for a in rd] + [(a, True) for a in wr]:
+                for j, other, o_w in by.get(mine[0], []):
+                    ps = mine[0] == "ps"
+                    if ps and lane[j] == lane[i] and (lane[i] == "pe" or not (is_w or o_w)):
+                        continue
+                    if (is_w or o_w or ps) and _meet(mine, other):
+                        deps.add(j)
+            k = known[q]
+            for j in sorted(deps, reverse=True):
+                if k.get(lane[j], -1) < j:
+                    waits[i].append(j)
+                    wanted.add(j)
+                    for a, b in clock[j].items():
+                        if k.get(a, -1) < b:
+                            k[a] = b
+            clock[i] = dict(k)
+            clock[i][lane[i]] = i
+        for a in rd:
+            by.setdefault(a[0], []).append((i, a, False))
+        for a in wr:
+            by.setdefault(a[0], []).append((i, a, True))
+    last = {}
+    for i, o in enumerate(ops):
+        if o[1] == "c":
+            last[o[0]] = i
+    wanted.update(last.values())
+    mark, count, nd = {}, {q: 0 for q in queues}, 0
+    for i, (q, kind, call, rd, wr) in enumerate(ops):
+        if kind == "c" and i in wanted:
+            count[q] += 1
+            mark[i] = (q, count[q])
+        elif kind == "a":
+            mark[i] = call
+        elif kind != "c":
+            mark[i] = ("d%d" % nd, call[1])
+            nd += 1
+    for i, (q, kind, call, rd, wr) in enumerate(ops):
+        if kind == "a":
+            continue
+        for j in waits[i]:
+            queues[q].wait_ge(T.sem[mark[j][0]], mark[j][1])
+        if kind == "c":
+            ins = call(queues[q])
+            if i in mark:
+                ins.then_inc(T.sem[q], 1)
+        else:
+            call[0](queues[q], T.sem[mark[i][0]])
+    for i, o in enumerate(ops):
+        if o[1] != "c" or last[o[0]] == i:
+            g.wait_ge(T.sem[mark[i][0]], mark[i][1])
+
+
+def rank_program(g, core, T, topo):
+    r = T.rank_of(core)
+    if r is None:
+        return
+    ALU, ACT = AluOpType, ActivationFunctionType
+    ops = []
+
+    def ap(a):
+        if isinstance(a, (int, float)) or a is None:
+            return a
+        if a[0] == "@":
+            return ap(a[1]).indirect(ap(a[2]))
+        return T[a[0]][a[1]:a[2], a[3]:a[4]:a[5]] if a[5] != 1 else T[a[0]][a[1]:a[2], a[3]:a[4]]
+
+    def regs(*xs):
+        out = []
+        for a in xs:
+            if isinstance(a, tuple):
+                out += [a[1], a[2]] if a[0] == "@" else [a]
+        return out
+
+    def ind(win, off):
+        return ("@", win, off)
+
+    def comp(q, call, rd, wr):
+        ops.append([q, "c", call, rd, wr])
+
+    def memset(o, v):
+        comp("ve", lambda e: e.memset(ap(o), v), [], [o])
+
+    def copy(o, i):
+        if o[0] == "@":
+            comp("ve", lambda e: e.tensor_copy(ap(o), ap(i)), [i, o[2]], [o[1]])
+        else:
+            comp("ve", lambda e: e.tensor_copy(ap(o), ap(i)), regs(i), [o])
+
+    def tt(o, a, b, op):
+        comp("ve", lambda e: e.tensor_tensor(ap(o), ap(a), ap(b), op), regs(a, b), [o])
+
+    def ts(o, a, s1, op0, s2=None, op1=None):
+        if op1 is None:
+            comp("ve", lambda e: e.tensor_scalar(ap(o), ap(a), ap(s1), None, op0), regs(a, s1), [o])
+        else:
+            comp("ve", lambda e: e.tensor_scalar(ap(o), ap(a), ap(s1), ap(s2), op0, op1), regs(a, s1, s2), [o])
+
+    def scan(o, a, b, init, op0, op1):
+        comp("ve", lambda e: e.tensor_tensor_scan(ap(o), ap(a), ap(b), ap(init), op0, op1), regs(a, b, init), [o])
+
+    def turn(o, i):
+        comp("ve", lambda e: e.transpose(ap(o), ap(i)), [i], [o])
+
+    def quant(qo, so, i):
+        comp("ve", lambda e: e.quantize_mx(ap(qo), ap(so), ap(i)), [i], [qo, so])
+
+    def act(o, i, f, bias=0.0, scale=1.0, acc=None):
+        if acc is None:
+            comp("se", lambda e: e.activation(ap(o), ap(i), f, bias=ap(bias), scale=scale), regs(i, bias), [o])
+        else:
+            comp("se", lambda e: e.activation(ap(o), ap(i), f, bias=ap(bias), scale=scale, accum_out=ap(acc)), regs(i, bias), [o, acc])
+
+    def actcopy(o, i):
+        comp("se", lambda e: e.activation(ap(o), ap(i), ACT.Copy), regs(i), [o])
+
+    def fill(o, v):
+        act(o, A("one", 0, len(range(o[3], o[4], o[5])), 1, o[1], o[2]), ACT.Identity, scale=float(v))
+
+    def mm(o, lq, ls, rq, rs):
+        comp("pe", lambda e: e.matmul_mx(ap(o), ap(lq), ap(ls), ap(rq), ap(rs), True, True), [lq, ls, rq, rs], [o])
+
+    def unpack(o, b, q, s):
+        mm(o, A("eq", 128 * b, 128 * b + 128), A("es", 128 * b, 128 * b + 128), q, s)
+
+    def layer(o, b, q, s):
+        mm(o, A("wq", 128 * b, 128 * b + 128), A("wsc", 128 * b, 128 * b + 128), q, s)
+
+    def iota(o, pat, base):
+        comp("ge", lambda e: e.iota(ap(o), pat, base, 0, allow_small_or_imprecise_dtypes=True), [], [o])
+
+    def dma(q, out, in_, rd, wr):
+        ops.append([q, "d", (lambda e, s: e.dma_start(out, in_).then_inc(s, 16), 16), rd, wr])
+
+    def b8(a):
+        return ap(a).bitcast(dt.uint8)
+
+    def dst(k):
+        a = topo.addr(T.cores[k])
+        return DstId(rid=a[0], pnc=a[1])
+
+    def masks(k, parts):
+        e = topo.engines(core, T.cores[k])
+        w = len(e) // parts
+        return [sum(1 << x for x in e[i * w:(i + 1) * w]) for i in range(parts)], w
+
+    def send_sides(sem, pieces):
+        ms, w = masks(pieces[0][0], 2)
+        form = lambda a, y: b8(a) if y else ap(a)
+
+        def call(e, s):
+            e.remote_dma_fused([RemoteDMATransfer(dst_ids=[dst(k)], dma_engine_mask=ms[0 if k < r else 1], remote_sem=T.sem[sem],
+                                                  src=form(a, y), dst=form(b, y)) for k, a, b, y in pieces], local_sem=s)
+        ops.append(["ge", "d", (call, w * len(pieces)), [p[1] for p in pieces], []])
+        return w
+
+    def arrive(sem, n, wr):
+        ops.append(["", "a", (sem, n), [], wr])
+
+    left, right = r > 0, r < N - 1
+    sides = int(left) + int(right)
+    base = 0 if r < N // 2 else N // 2
+    extra = {N // 2 - 1: N // 2, N // 2: N // 2 - 1}.get(r)
+    nc = 1 if extra is None else 2
+    ranks = list(range(0, r + 2)) if r < N // 2 else list(range(r - 1, N))
+    nr = 32 * len(ranks)
+    ns = 48
+    back = -(-S * r // (L + 1)) if r <= N // 2 else -(-S * (N - r) // (L - 1))
+    s0 = 16 - back if right else 0
+    s1 = s0 + ns
+    w0 = 32 * ranks.index(r) - 16 + s0
+    nb0 = (L * (16 - s0) + min(128, 32 * r) + 15) // 16 if left else 1
+    nscan = 5 * (nb0 + 28)
+    col = lambda k, at=r: 0 if k == at else 4 + k - int(k > at)
+    kcol, m4b, inic = [A("cf", j, j + 1) for j in range(3)]
+    icol, m4a = A("pk", 0, 1), A("pk", 2, 3)
+    zer = A("zer", 0, 32)
+
+    cuts = [(0, BW), (C - BW, C), (BW, C - BW)]
+    for j, (a, b) in enumerate(cuts):
+        dma("se" if j == 1 else "sy", ap(A("xt", 4 * a, 4 * b)), T.x[:, 4 * a:4 * b], [], [A("xt", 4 * a, 4 * b)])
+    dma("se", ap(A("ut", 0, 512)), T.u[:], [], [A("ut", 0, 512)])
+    dma("sy", b8(A("wq", 0, 512)), T.wc[:], [A("xt", 0, 4 * C), A("ut", 0, 512)], [A("wq", 0, 512)])
+    dma("sy", ap(A("wsc", 0, 512)), T.ws[:], [], [A("wsc", 0, 512)])
+
+    comp("ge", lambda e: e.iota(ap(A("pi", 0, 8)), [[0, 8]], 0, 1), [], [A("pi", 0, 8)])
+    memset(A("one", 0, 512), 1.0)
+    memset(A("eb", 0, 1040), 0.0)
+    comp("ge", lambda e: e.affine_select(ap(A("idn", 0, 128)), ap(A("one", 0, 128)), [[-1, 128]], ALU.is_equal, 0.0, 0, 1),
+         [A("one", 0, 128)], [A("idn", 0, 128)])
+    iota(A("io16", 0, 112), [[0, 7], [1, 16]], 0)
+    iota(A("hc", 0, 64), [[1, 64]], FW - BW - 1)
+    iota(A("fo", 6, 10), [[1, 4]], 0)
+    ts(A("pj", 0, 8), A("pi", 0, 8), 7, ALU.bitwise_and)
+    memset(A("d0", 0, 512), 1.0)
+    ts(A("uoff", 0, 8), A("pj", 0, 8), 16.0, ALU.mult)
+    ts(A("pj", 0, 1), A("pi", 0, 1), 15, ALU.bitwise_and)
+    ts(A("pj", 1, 2), A("pi", 0, 1), 31, ALU.bitwise_and)
+    ts(A("pj", 2, 3), A("pi", 0, 1), 3, ALU.bitwise_and)
+    ts(A("pj", 3, 4), A("pi", 0, 1), 5, ALU.arith_shift_right)
+    copy(A("pk", 0, 4), A("pj", 0, 4))
+    actcopy(A("eb", 2, 514, 4), A("idn", 0, 128))
+    actcopy(A("eb", 523, 1035, 4), A("idn", 0, 128))
+    for b in range(4):
+        c0 = 520 * (b % 2) + 2 - 2 * (b // 2)
+        quant(A("eq", 128 * b, 128 * b + 128), A("es", 128 * b, 128 * b + 128), A("eb", c0, c0 + 512))
+    fill(A("om", 0, 416, 2), 0.0)
+    fill(A("d1", 0, 256, 2), 0.0)
+    fill(A("om", 1, 416, 32), BIG)
+    fill(A("om", 31, 416, 32), BIG)
+    memset(A("neg", 0, 32), -1.0)
+    memset(A("dp", 0, 160), 0.0)
+    memset(A("bn", 0, 96), 0.0)
+    for a, b in cuts[:2]:
+        quant(A("t0", a, b), A("s0", a, b), A("xt", 4 * a, 4 * b))
+    quant(A("uq", 0, 128), A("us", 0, 128), A("ut", 0, 512))
+    comp("ve", lambda e: e.tensor_copy(ap(A("uq2", 0, 128)).bitcast(dt.uint32), ap(A("uq", 0, 128)).bitcast(dt.uint32).indirect(ap(A("uoff", 0, 8)))),
+         [A("uq", 0, 128), A("uoff", 0, 8)], [A("uq2", 0, 128)])
+    quant(A("t0", BW, C - BW), A("s0", BW, C - BW), A("xt", 4 * BW, 4 * (C - BW)))
+    act(A("thc", 0, 96), A("io16", 0, 96), ACT.Identity, bias=-8.0)
+    act(A("thc", 96, 112), A("io16", 96, 112), ACT.Identity, bias=-1.5)
+    act(A("cf", 5, 6), icol, ACT.Identity, scale=-1.0)
+    act(kcol, A("pk", 1, 2), ACT.Identity, bias=6.5, scale=float(L))
+    act(m4b, m4a, ACT.Identity, bias=float(WOFF + 5))
+    act(inic, icol, ACT.Identity, bias=float(BW - 16 - (0 if left else 16 * nb0)))
+    act(A("rt0", 0, 64), A("io16", 0, 64), ACT.Abs, bias=A("cf", 5, 6))
+    for c in range(2):
+        act(A("fo", 2 + c, 3 + c), A("pk", 3, 4), ACT.Identity, bias=float(c), scale=2.0)
+        act(A("fo", 4 + c, 5 + c), A("pk", 3, 4), ACT.Identity, bias=m4a, scale=2.0)
+    fill(A("nst", 9, 10), 0.0)
+    act(A("rt", 0, 64), A("rt0", 0, 64), ACT.Relu, bias=1.0e6, scale=-1.0e6)
+    fill(A("fo", 1, 2), col(base if extra is None else extra))
+    fill(zer, 0.0)
+    act(A("d0", 32 * base, 32 * base + 128), A("idn", 0, 128), ACT.Identity, bias=1.0, scale=-2.0)
+    if extra is not None:
+        for a in range(4):
+            act(A("d0", 256 + 32 * extra, 288 + 32 * extra, 1, 32 * a, 32 * a + 32), A("idn", 32 * a, 32 * a + 32, 1, 32 * a, 32 * a + 32),
+                ACT.Identity, bias=1.0, scale=-2.0)
+    actcopy(A("us2", 0, 128), ind(A("us", 0, 128), A("uoff", 0, 8)))
+    for a in range(4):
+        fill(A("fo", 0, 1, 1, 32 * a, 32 * a + 32), col(base + a))
+    for t in range(R):
+        fill(A("vtl%d" % t, 4 * ns, 512), 0.0)
+        fill(A("lc%d" % t, 1, 4), 0.0)
+
+    for t in range(R):
+        n = lambda s: s + str(t)
+        tq, tsc, fh = n("t"), n("s"), n("fh")
+        pc, psc = [], []
+        if left:
+            pc.append((r - 1, A(tq, 0, BW), A(n("lt"), BW, 2 * BW), True))
+            psc.append((r - 1, A(tsc, 0, BW), A(n("ls"), BW, 2 * BW), False))
+        if right:
+            pc.append((r + 1, A(tq, C - BW, C), A(n("lt"), 0, BW), True))
+            psc.append((r + 1, A(tsc, C - BW, C), A(n("ls"), 0, BW), False))
+        w = send_sides(n("at"), pc)
+        send_sides(n("at"), psc)
+        l0, l1 = (0 if left else BW), (2 * BW if right else BW)
+        arrive(n("at"), 2 * w * sides, [A(n("lt"), l0, l1), A(n("ls"), l0, l1)])
+        mm(bank(0, C), A("uq2", 0, 128), A("us2", 0, 128), A(tq, 0, C), A(tsc, 0, C))
+        for b in range(4):
+            unpack(bank(1 + b, C), b, A(tq, 0, C), A(tsc, 0, C))
+        if t == R - 1:
+            quant(A("vq", 0, 128), A("vs", 0, 128), A("vt", 0, 512))
+        for l in range(L):
+            turn(A("et", 32 * l, 32 * l + 32), A("ps", l, C, L))
+        fown = lambda b: actcopy(A(fh, PW * b + BW, PW * b + BW + C), bank(1 + b, C))
+        fown(0)
+        m = lambda a, b: A("om", 2 * a + 1, 2 * b + 1, 2)
+        low = lambda a, b: A("d1", 2 * a, 2 * b, 2)
+        e_to = lambda row, k: act(A("d1", 32 * row + 1, 32 * row + 28, 2), A("et", k, C, 32), ACT.Abs)
+        pair = lambda row, frm: tt(low(16 * row, 16 * row + 15), m(16 * frm, 16 * frm + 15), m(16 * frm + 1, 16 * frm + 16), ALU.min)
+        wipe = lambda row: memset(A("om", 32 * row + 2, 32 * row + 30, 2), 0.0)
+        step = lambda row, frm: scan(A("om", 32 * row + 2, 32 * row + 30), A("om", 32 * frm + 4, 32 * frm + 32), A("d1", 32 * row, 32 * row + 28),
+                                     0.0, ALU.min, ALU.max)
+        act(m(1, 15), A("et", 0, C, 32), ACT.Abs)
+        act(m(129, 143), A("et", 7, C, 32), ACT.Abs)
+        for row, k in ((1, 1), (9, 6), (2, 2), (10, 5), (3, 3), (11, 4), (4, 4), (5, 5), (6, 6), (7, 7)):
+            e_to(row, k)
+        fown(1)
+        fown(2)
+        fill(A(n("win"), 0, nscan), 0.0)
+        fill(A(n("win"), WOFF, WOFF + nscan), 0.0)
+        fill(A(n("win"), 4, nscan, 5), 16.0)
+        for k in range(1, 4):
+            pair(k, k - 1)
+            if k > 1:
+                wipe(k - 1)
+            pair(8 + k, 7 + k)
+            if k > 1:
+                wipe(7 + k)
+            step(k, k - 1)
+            step(8 + k, 7 + k)
+        pair(12, 3)
+        wipe(3)
+        copy(A("d1", 32 * 12 + 1, 32 * 12 + 28, 2), m(177, 191))
+        pair(4, 3)
+        step(12, 3)
+        step(4, 3)
+        scan(A(n("pm"), 0, L), m(193, 207), m(193, 207), BIG, ALU.min, ALU.min)
+        cost = A(n("pm"), L - 1, L)
+        others = [(r + d) % N for d in range(1, N)]
+        full, wf = masks(others[0], 1)
+
+        def send_costs(e, s, t=t, cost=cost, full=full, others=others):
+            e.remote_dma_fused([RemoteDMATransfer(dst_ids=[dst(k) for k in others], dma_engine_mask=full[0], remote_sem=T.sem["ac%d_%d" % (t, r)],
+                                                  srcs=[ap(cost)], dsts=[ap(A("lc%d" % t, col(r, k), col(r, k) + 1)) for k in others])], local_sem=s)
+        ops.append(["ge", "d", (send_costs, wf), [cost], []])
+        for k in others:
+            arrive("ac%d_%d" % (t, k), wf, [A(n("lc"), col(k), col(k) + 1)])
+        actcopy(A(n("lc"), 0, 1), cost)
+        act(A("bc", 32 * r, 32 * r + 32), zer, ACT.Identity, bias=cost)
+        tx = lambda a, b: tt(A("tx", a, b), m(a, b), low(a + 17, b + 17), ALU.is_le)
+        ty = lambda a, b: tt(A("ty", a, b), low(a + 15, b + 15), m(a + 1, b + 1), ALU.is_le)
+        tz = lambda a, b: tt(A("tz", a, b), A("tx", a, b), A("thc", a, b), ALU.add)
+        th = lambda a, b: tt(A("th", a, b), A("tz", a, b), A("ty", a, b), ALU.add)
+        if t == 0:
+            copy(A("off", 0, 10), A("fo", 0, 10))
+        for k, gap in ((5, (tx, ty)), (6, (tz, th)), (7, ())):
+            pair(k, k - 1)
+            wipe(k - 1)
+            for f in gap[:1]:
+                f(1, 62)
+            step(k, k - 1)
+            for f in gap[1:]:
+                f(1, 62)
+        tx(65, 110)
+        scan(A("pc", 0, L), m(113, 127), m(113, 127), BIG, ALU.min, ALU.min)
+        ty(65, 110)
+        tz(65, 110)
+        act(A("junk2", 0, L), A("pc", 0, L), ACT.Sign, bias=cost, scale=-1.0, acc=A("nst", 8, 9))
+        th(65, 110)
+        copy(A(fh, PW * 3 + BW, PW * 3 + BW + C), bank(4, C))
+        turn(A("aa", 32 * r, 32 * r + 32), A("bc", 32 * r, 32 * r + 32))
+        if sides == 1:
+            for b in range(4):
+                c0 = PW * b + (0 if not left else BW + C)
+                memset(A(fh, c0, c0 + BW), 0.0)
+        act(A("nst", 7, 8), A("nst", 8, 9), ACT.Identity, bias=13.0, scale=2.0)
+        for k in range(7, 0, -1):
+            o = 16 * (k - 1)
+            act(A("junk2", 16 * k, 16 * k + L - 1), A("th", o + 1, o + L), ACT.Sign, bias=A("nst", 8, 9) if k == 7 else A("nst", k, k + 1),
+                scale=1.0 if k == 7 else 2.0, acc=A("nst", k - 1, k))
+        act(A(n("pw"), 0, 16), ind(A("nst", 0, 10), A("off", 4, 5)), ACT.Identity, bias=kcol, scale=-0.5)
+        pp = []
+        if left:
+            pp.append((r - 1, A(n("pw"), 0, 2), A(n("lp"), 2, 4) if r > 1 else A(n("lp"), 0, 2), False))
+        if right:
+            pp.append((r + 1, A(n("pw"), 0, 2), A(n("lp"), 0, 2), False))
+        w = send_sides(n("ap"), pp)
+        arrive(n("ap"), w * sides, [A(n("lp"), 0, 2 * sides)])
+        act(A("bn", 32, 64), ind(A("nst", 0, 8), A("off", 2, 4)), ACT.Identity, bias=kcol, scale=-0.5)
+        for b in range(4):
+            unpack(bank(1 + b, l1 - l0), b, A(n("lt"), l0, l1), A(n("ls"), l0, l1))
+            move = copy if b < 3 else actcopy
+            if left:
+                move(A(fh, PW * b, PW * b + BW), bank(1 + b, BW))
+            if right:
+                c0 = 512 * (1 + b) + (BW if left else 0)
+                move(A(fh, PW * b + BW + C, PW * b + FW), A("ps", c0, c0 + BW))
+        for k in others[::-1]:
+            act(A("bc", 32 * k, 32 * k + 32), zer, ACT.Identity, bias=A(n("lc"), col(k), col(k) + 1))
+            turn(A("aa", 32 * k, 32 * k + 32), A("bc", 32 * k, 32 * k + 32))
+        actcopy(A("bc", 256, 288), ind(A(n("lc"), 0, 11), A("off", 0, 2)))
+        if t == 0:
+            dma("sy", ap(A("vt", 0, 512)), T.v[:], [A("bc", 256, 288)], [A("vt", 0, 512)])
+        for c in range(nc):
+            v = A("bc", 256 + 16 * c, 257 + 16 * c)
+            act(A("junk", 256 * c, 256 * c + 256), A("aa", 0, 256), ACT.Sign, bias=v, scale=-1.0, acc=A("pp", c, c + 1))
+            ts(A("eqt", 256 * c, 256 * c + 256), A("aa", 0, 256), v, ALU.is_equal)
+        for c in range(nc):
+            scan(A("sct", 256 * c, 256 * c + 256), A("d0", 256 * c, 256 * c + 256), A("eqt", 256 * c, 256 * c + 256), 0.0, ALU.mult, ALU.add)
+        for c in range(nc):
+            ts(A("fl", c, c + 1), A("pp", c, c + 1), A("sct", 256 * c + 255, 256 * c + 256), ALU.is_ge, 2.0, ALU.mult)
+        turn_no = 0
+        for j, k in enumerate(ranks):
+            if k == extra:
+                continue
+            a = k - base
+            for q in range(4):
+                o, i, f = A("bfl", 32 * j, 32 * j + 32, 1, 32 * q, 32 * q + 32), A("neg", 0, 32, 1, 32 * a, 32 * a + 32), A("fl", 0, 1, 1, 32 * a, 32 * a + 32)
+                if turn_no % 2:
+                    ts(o, i, f, ALU.add)
+                else:
+                    act(o, i, ACT.Identity, bias=f)
+                turn_no += 1
+        if extra is not None:
+            j = ranks.index(extra)
+            ts(A("bfl", 32 * j, 32 * j + 32), A("neg", 0, 32), A("fl", 1, 2), ALU.add)
+        pfw = A(n("pf"), 16 + s0, 16 + s1)
+        lp = A(n("lp"), 0, 2 * sides)
+        if left:
+            act(A("bn", 0, 32), ind(lp, A("off", 6, 8)), ACT.Identity, bias=float(-C))
+        if right:
+            act(A("bn", 64, 96), ind(lp, A("off", 8, 10) if left else A("off", 6, 8)), ACT.Identity, bias=float(C))
+        turn(A("sd", 0, nr), A("bfl", 0, nr))
+        sdw = A("sd", w0, w0 + ns)
+        act(A("dr", 0, ns), sdw, ACT.Identity, bias=0.5, scale=0.5)
+        scan(A("zs", 0, w0 + ns), A("sd", 0, w0 + ns), A("dp", 0, w0 + ns), 16.0 * nb0, ALU.add, ALU.add)
+        if base:
+            comp("ve", lambda e: e.tensor_reduce(ap(A("tot", 0, 1)), ap(A("sd", 0, nr)), AxisListType.X, ALU.add), [A("sd", 0, nr)], [A("tot", 0, 1)])
+        tot = A("tot", 0, 1) if base else 0.0
+        turn(A(n("pf"), 0, 96), A("bn", 0, 96))
+        if t == R - 1:
+            dma("sy", T.ol[:], T[n("pf")][0:128:16, 32:64], [A(n("pf"), 32, 64)], [])
+        zw = A("zz", 0, ns)
+        tt(zw, A("zs", w0, w0 + ns), pfw, ALU.add)
+        scan(A("wp", 0, ns), A("rt", 0, ns), pfw, 0.0, ALU.add, ALU.min)
+        tt(A("hd", 0, ns), A("hc", 0, ns), pfw, ALU.subtract)
+        ts(A(n("voff"), 0, 3), A("wp", 15, ns, 16), float(BW), ALU.add, *((float(FW - 1), ALU.min) if right else (0.0, ALU.max)))
+        for b in range(4):
+            actcopy(A(n("vtl"), b, 4 * ns, 4), ind(A(fh, PW * b, PW * b + FW), A(n("voff"), 0, 3)))
+        n4 = ns // 16
+        ts(A("zi", 0, ns), zw, tot, ALU.subtract)
+        scan(A("wz", 0, ns), A("rt", 0, ns), zw, 0.0, ALU.add, ALU.min)
+        if base:
+            act(A("ini", 1, 2), tot, ACT.Identity, bias=inic)
+        if left:
+            act(A("ini", 0, 1), A("zs", w0 - 1, w0), ACT.Identity, bias=A("ini", 1, 2) if base else inic, scale=-1.0)
+        ini = A("ini", 0, 1) if left else inic
+        ts(A("zb", 0, ns), A("zi", 0, ns), 15, ALU.bitwise_and)
+        ts(A("wi", 0, n4), A("wz", 15, ns, 16), tot, ALU.subtract)
+        tt(A("dh", 0, ns), A("dr", 0, ns), A("hd", 0, ns), ALU.mult)
+        ts(A("e1", 0, ns), A("zb", 0, ns), icol, ALU.is_equal)
+        ts(A("e2", 0, ns), A("zb", 0, ns), icol, ALU.is_lt)
+        ts(A("wa", 0, n4), A("wi", 0, n4), 4, ALU.arith_shift_right)
+        tt(A("x1", 0, ns), A("e1", 0, ns), A("dh", 0, ns), ALU.mult)
+        tt(A("x2", 0, ns), A("e2", 0, ns), sdw, ALU.mult)
+        ts(A("so", 0, n4), A("wa", 0, n4), 5.0, ALU.mult, m4a, ALU.add)
+        quant(A(n("qv"), 0, 128), A(n("sv"), 0, 128), A(n("vtl"), 0, 512))
+        for b in range(4):
+            layer(bank(1 + b, 128), b, A(n("qv"), 0, 128), A(n("sv"), 0, 128))
+            act(A(fh, PW * b + FW, PW * b + PW), bank(1 + b, ns), ACT.Relu, scale=0.03125)
+        tt(A("vv", 0, ns), A("x1", 0, ns), A("x2", 0, ns), ALU.subtract)
+        ts(A("so", n4, 2 * n4), A("wa", 0, n4), 5.0, ALU.mult, m4b, ALU.add)
+        tt(A("vv", ns, 2 * ns), A("vv", 0, ns), sdw, ALU.add)
+        copy(ind(A(n("win"), 0, 2 * WOFF), A("so", 0, 2 * n4)), A("vv", 0, 2 * ns))
+        scan(A("sc", 0, nscan), A(n("win"), 0, nscan), A(n("win"), WOFF, WOFF + nscan), ini, ALU.add, ALU.subtract)
+        copy(A(n("eoff"), 0, 28), A("sc", 5 * nb0 + 4, nscan, 5))
+        nq, nsc = "t%d" % (t + 1), "s%d" % (t + 1)
+        cols = lambda name, h: A(name, HALF * h, HALF * h + HALF)
+        plane = lambda name, h, b: A(name, 4 * HALF * h + b, 4 * HALF * (h + 1), 4)
+        src = lambda h, b: ind(A(fh, PW * b, PW * b + PW), A(n("eoff"), 14 * h, 14 * h + 14))
+        etl, xn = n("etl"), n("xn")
+        qe = lambda h: quant(cols(n("qe"), h), cols(n("se"), h), A(etl, 4 * HALF * h, 4 * HALF * (h + 1)))
+        rl = lambda h, b: A("rl", HALF * (4 * h + b), HALF * (4 * h + b + 1))
+
+        def products(h, b):
+            layer(bank(4 + b, HALF), b, cols(n("qe"), h), cols(n("se"), h))
+            unpack(bank(b, HALF), b, cols(n("qe"), h), cols(n("se"), h))
+        for b in range(2):
+            copy(plane(etl, 0, b), src(0, b))
+            actcopy(plane(etl, 0, 2 + b), src(0, 2 + b))
+        qe(0)
+        for b in range(4):
+            products(0, b)
+        copy(plane(etl, 1, 0), src(1, 0))
+        for b in range(1, 4):
+            actcopy(plane(etl, 1, b), src(1, b))
+        ts(rl(0, 0), bank(4, HALF), 0.0, ALU.max, 0.015625, ALU.mult)
+        for h in range(2):
+            for b in range(4):
+                if h or b:
+                    act(rl(h, b), bank(4 + b, HALF), ACT.Relu, scale=0.015625)
+                tt(plane(xn, h, b), bank(b, HALF), rl(h, b), ALU.add)
+                if h == 0:
+                    if b == 0:
+                        qe(1)
+                    products(1, b)
+            quant(cols(nq, h), cols(nsc, h), A(xn, 4 * HALF * h, 4 * HALF * (h + 1)))
+
+    for h in range(2):
+        c0, c1 = HALF * h, HALF * h + HALF
+        dma("sy", T.oc[:, 4 * c0:4 * c1], b8(A("t2", c0, c1)), [A("t2", c0, c1)], [])
+        mm(bank(h, HALF), A("vq", 0, 128), A("vs", 0, 128), A("t2", c0, c1), A("s2", c0, c1))
+        actcopy(A("ys", c0, c1), bank(h, HALF))
+        dma("se", T.y[:, c0:c1], ap(A("ys", c0, c1)), [A("ys", c0, c1)], [])
+    for k in range(4):
+        dma("sy", T.osc[4 * k:4 * k + 4, 0:C], T.s2[32 * k:32 * k + 4, 0:C], [A("s2", 0, C)], [])
+    emit(g, T, ops)

@@ -13,19 +13,15 @@ Q4, U8, BF, F32, I32, U16 = "float8_e4m3fn_x4", "uint8", "bfloat16", "float32", 
 SCRATCH = {"ps": ("psum", [128, 4096], F32)}
 for _n, _w, _d in [("xt", 4 * C, BF), ("ut", 512, BF), ("vt", 512, BF), ("uq", 128, Q4), ("us", 128, U8), ("uq2", 128, Q4),
                    ("us2", 128, U8), ("vq", 128, Q4), ("vs", 128, U8), ("wq", 512, Q4), ("wsc", 512, U8), ("eb", 1040, BF),
-                   ("eq", 512, Q4), ("es", 512, U8), ("one", 512, BF), ("pk", 8, F32), ("fo", 10, F32), ("off", 10, U16),
-                   ("zz", 64, F32), ("idn", 128, BF), ("pi", 8, I32), ("pj", 8, I32), ("cf", 8, F32), ("uoff", 8, U16),
-                   ("rt", 64, F32), ("io16", 112, F32), ("thc", 112, F32), ("hc", 64, F32), ("d0", 512, BF), ("zer", 32, F32),
-                   ("neg", 32, F32), ("om", 416, F32), ("d1", 416, F32), ("pc", 16, F32), ("et", C, F32), ("tx", 112, F32),
-                   ("ty", 112, F32), ("tz", 112, F32), ("th", 112, F32), ("junk", 512, BF), ("junk2", 128, F32),
-                   ("nst", 16, F32), ("rt0", 64, F32),
-                   ("bc", 288, F32), ("aa", 256, F32), ("eqt", 512, BF), ("sct", 512, BF), ("pp", 4, F32), ("fl", 4, F32),
-                   ("bfl", 160, F32), ("sd", 160, F32), ("dp", 160, F32), ("zs", 160, F32), ("tot", 4, F32), ("bn", 96, F32),
-                   ("wp", 64, F32), ("hd", 64, F32), ("dr", 64, F32), ("dh", 64, F32), ("zi", 64, I32), ("zb", 64, I32),
-                   ("e1", 64, F32), ("e2", 64, F32), ("x1", 64, F32), ("x2", 64, F32), ("vv", 128, F32), ("wz", 64, F32),
-                   ("wi", 4, I32), ("wa", 4, I32), ("so", 8, U16), ("ini", 4, F32), ("sc", WOFF, F32), ("rl", 8 * HALF, F32),
-                   ("ys", C, F32), ("t2", C, Q4), ("s2", C, U8)]:
+                   ("eq", 512, Q4), ("es", 512, U8), ("one", 512, BF), ("idn", 128, BF), ("d0", 512, BF), ("junk", 512, BF),
+                   ("eqt", 512, BF), ("sct", 512, BF), ("off", 8, U16), ("uoff", 8, U16), ("so", 8, U16), ("pi", 8, I32),
+                   ("pj", 8, I32), ("zi", 64, I32), ("zb", 64, I32), ("wi", 4, I32), ("wa", 4, I32), ("t2", C, Q4), ("s2", C, U8)]:
     SCRATCH[_n] = ("sbuf", [128, _w], _d)
+for _w, _ns in [(4, "pp fl tot ini"), (8, "pk fo cf"), (16, "pc nst"), (32, "zer neg"), (48, "g1 g2 df u1 u2 u3 th2"),
+                (64, "zz zt rt rt0 hc wp hd dr dh e1 e2 x1 x2 x3 wz"), (96, "bn"), (112, "io16 thc tx ty tz th"), (128, "junk2 vv"),
+                (160, "bfl sd dp zs"), (256, "aa"), (288, "bc"), (WOFF, "sc"), (416, "om d1"), (C, "et ys"), (8 * HALF, "rl")]:
+    for _n in _ns.split():
+        SCRATCH[_n] = ("sbuf", [128, _w], F32)
 for _t in range(R):
     for _n, _w, _d in [("t", C, Q4), ("s", C, U8), ("lt", 2 * BW, Q4), ("ls", 2 * BW, U8), ("fh", 4 * PW, BF), ("pm", 16, F32),
                        ("lc", 16, F32), ("lp", 4, F32), ("pf", 96, F32), ("pw", 16, F32), ("voff", 4, U16), ("vtl", 512, BF),
@@ -258,15 +254,14 @@ def rank_program(g, core, T, topo):
          [A("one", 0, 128)], [A("idn", 0, 128)])
     iota(A("io16", 0, 112), [[0, 7], [1, 16]], 0)
     iota(A("hc", 0, 64), [[1, 64]], FW - BW - 1)
-    iota(A("fo", 6, 10), [[1, 4]], 0)
+    iota(A("fo", 2, 6), [[1, 4]], 0)
     ts(A("pj", 0, 8), A("pi", 0, 8), 7, ALU.bitwise_and)
     memset(A("d0", 0, 512), 1.0)
     ts(A("uoff", 0, 8), A("pj", 0, 8), 16.0, ALU.mult)
     ts(A("pj", 0, 1), A("pi", 0, 1), 15, ALU.bitwise_and)
     ts(A("pj", 1, 2), A("pi", 0, 1), 31, ALU.bitwise_and)
     ts(A("pj", 2, 3), A("pi", 0, 1), 3, ALU.bitwise_and)
-    ts(A("pj", 3, 4), A("pi", 0, 1), 5, ALU.arith_shift_right)
-    copy(A("pk", 0, 4), A("pj", 0, 4))
+    copy(A("pk", 0, 3), A("pj", 0, 3))
     actcopy(A("eb", 2, 514, 4), A("idn", 0, 128))
     actcopy(A("eb", 523, 1035, 4), A("idn", 0, 128))
     for b in range(4):
@@ -292,10 +287,8 @@ def rank_program(g, core, T, topo):
     act(m4b, m4a, ACT.Identity, bias=float(WOFF + 5))
     act(inic, icol, ACT.Identity, bias=float(BW - 16 - (0 if left else 16 * nb0)))
     act(A("rt0", 0, 64), A("io16", 0, 64), ACT.Abs, bias=A("cf", 5, 6))
-    for c in range(2):
-        act(A("fo", 2 + c, 3 + c), A("pk", 3, 4), ACT.Identity, bias=float(c), scale=2.0)
-        act(A("fo", 4 + c, 5 + c), A("pk", 3, 4), ACT.Identity, bias=m4a, scale=2.0)
-    fill(A("nst", 9, 10), 0.0)
+    act(A("cf", 6, 7), A("pk", 1, 2), ACT.Identity, bias=6.5 - C, scale=float(L))
+    act(A("cf", 7, 8), A("pk", 1, 2), ACT.Identity, bias=6.5 + C, scale=float(L))
     act(A("rt", 0, 64), A("rt0", 0, 64), ACT.Relu, bias=1.0e6, scale=-1.0e6)
     fill(A("fo", 1, 2), col(base if extra is None else extra))
     fill(zer, 0.0)
@@ -345,8 +338,8 @@ def rank_program(g, core, T, topo):
         act(m(129, 143), A("et", 7, C, 32), ACT.Abs)
         for row, k in ((1, 1), (9, 6), (2, 2), (10, 5), (3, 3), (11, 4), (4, 4), (5, 5), (6, 6), (7, 7)):
             e_to(row, k)
-        fown(1)
-        fown(2)
+        for b in range(1, 4):
+            fown(b)
         fill(A(n("win"), 0, nscan), 0.0)
         fill(A(n("win"), WOFF, WOFF + nscan), 0.0)
         fill(A(n("win"), 4, nscan, 5), 16.0)
@@ -377,39 +370,69 @@ def rank_program(g, core, T, topo):
         for k in others:
             arrive("ac%d_%d" % (t, k), wf, [A(n("lc"), col(k), col(k) + 1)])
         actcopy(A(n("lc"), 0, 1), cost)
-        act(A("bc", 32 * r, 32 * r + 32), zer, ACT.Identity, bias=cost)
+
+        def borrowed(b, move):
+            unpack(bank(1 + b, l1 - l0), b, A(n("lt"), l0, l1), A(n("ls"), l0, l1))
+            if left:
+                move(A(fh, PW * b, PW * b + BW), bank(1 + b, BW))
+            if right:
+                c0 = 512 * (1 + b) + (BW if left else 0)
+                move(A(fh, PW * b + BW + C, PW * b + FW), A("ps", c0, c0 + BW))
         tx = lambda a, b: tt(A("tx", a, b), m(a, b), low(a + 17, b + 17), ALU.is_le)
         ty = lambda a, b: tt(A("ty", a, b), low(a + 15, b + 15), m(a + 1, b + 1), ALU.is_le)
         tz = lambda a, b: tt(A("tz", a, b), A("tx", a, b), A("thc", a, b), ALU.add)
         th = lambda a, b: tt(A("th", a, b), A("tz", a, b), A("ty", a, b), ALU.add)
+        two = lambda o, a, b, op: tt(A(o, 1, 46), A(a[0], 1 + a[1], 46 + a[1]), A(b[0], 1 + b[1], 46 + b[1]), op)
         if t == 0:
-            copy(A("off", 0, 10), A("fo", 0, 10))
-        for k, gap in ((5, (tx, ty)), (6, (tz, th)), (7, ())):
+            copy(A("off", 0, 6), A("fo", 0, 6))
+        for k, gap in ((5, (tx, ty)), (6, (tz, th))):
             pair(k, k - 1)
             wipe(k - 1)
-            for f in gap[:1]:
-                f(1, 62)
+            gap[0](1, 63)
             step(k, k - 1)
-            for f in gap[1:]:
-                f(1, 62)
+            gap[1](1, 63)
+        pair(7, 6)
+        wipe(6)
+        two("g1", ("tx", 0), ("ty", 0), ALU.max)
+        step(7, 6)
         tx(65, 110)
-        scan(A("pc", 0, L), m(113, 127), m(113, 127), BIG, ALU.min, ALU.min)
         ty(65, 110)
+        scan(A("pc", 0, L), m(113, 127), m(113, 127), BIG, ALU.min, ALU.min)
         tz(65, 110)
         act(A("junk2", 0, L), A("pc", 0, L), ACT.Sign, bias=cost, scale=-1.0, acc=A("nst", 8, 9))
+        two("g2", ("tx", 0), ("ty", 0), ALU.min)
         th(65, 110)
-        copy(A(fh, PW * 3 + BW, PW * 3 + BW + C), bank(4, C))
+        tt(A("df", 1, 47), A("th", 17, 63), A("th", 16, 62), ALU.subtract)
+        spread = lambda k, c: ts(A("bc", 32 * k, 32 * k + 32), zer, c, ALU.add)
+        spread(r, cost)
+        two("u1", ("g1", 0), ("df", 0), ALU.mult)
+        two("u2", ("g2", 0), ("df", 1), ALU.mult)
         turn(A("aa", 32 * r, 32 * r + 32), A("bc", 32 * r, 32 * r + 32))
+        two("u3", ("u1", 0), ("th", 15), ALU.add)
+        two("th2", ("u3", 0), ("u2", 0), ALU.add)
+        borrowed(0, copy)
+        borrowed(1, copy)
         if sides == 1:
             for b in range(4):
                 c0 = PW * b + (0 if not left else BW + C)
                 memset(A(fh, c0, c0 + BW), 0.0)
-        act(A("nst", 7, 8), A("nst", 8, 9), ACT.Identity, bias=13.0, scale=2.0)
-        for k in range(7, 0, -1):
-            o = 16 * (k - 1)
-            act(A("junk2", 16 * k, 16 * k + L - 1), A("th", o + 1, o + L), ACT.Sign, bias=A("nst", 8, 9) if k == 7 else A("nst", k, k + 1),
-                scale=1.0 if k == 7 else 2.0, acc=A("nst", k - 1, k))
-        act(A(n("pw"), 0, 16), ind(A("nst", 0, 10), A("off", 4, 5)), ACT.Identity, bias=kcol, scale=-0.5)
+        pw = lambda q, c0, c1: A(n("pw"), c0, c1, 1, 32 * q, 32 * q + 32)
+        nst = lambda c0, c1, q=None: A("nst", c0, c1) if q is None else A("nst", c0, c1, 1, 32 * q, 32 * q + 32)
+
+        def back_to(k, frm, name, o, acc, p1=128):
+            act(A("junk2", 16 * k + 16, 16 * k + 29, 1, 0, p1), A(name, o + 1, o + L, 1, 0, p1), ACT.Sign, bias=A("nst", frm, frm + 1, 1, 0, p1),
+                scale=1.0 if frm == 8 else 2.0, acc=acc)
+        back_to(6, 8, "th", 96, nst(6, 7))
+        act(pw(3, 1, 2), nst(8, 9, 3), ACT.Identity, bias=13.0, scale=2.0)
+        back_to(5, 6, "th", 80, nst(5, 6))
+        actcopy(pw(3, 0, 1), nst(6, 7, 3))
+        back_to(4, 5, "th", 64, nst(4, 5))
+        back_to(2, 4, "th2", 32, nst(2, 3))
+        back_to(3, 4, "th", 48, nst(3, 4))
+        actcopy(pw(2, 0, 2), nst(4, 6, 2))
+        back_to(0, 2, "th2", 0, pw(0, 0, 1), 32)
+        back_to(1, 2, "th", 16, pw(0, 1, 2), 32)
+        actcopy(pw(1, 0, 2), nst(2, 4, 1))
         pp = []
         if left:
             pp.append((r - 1, A(n("pw"), 0, 2), A(n("lp"), 2, 4) if r > 1 else A(n("lp"), 0, 2), False))
@@ -417,19 +440,19 @@ def rank_program(g, core, T, topo):
             pp.append((r + 1, A(n("pw"), 0, 2), A(n("lp"), 0, 2), False))
         w = send_sides(n("ap"), pp)
         arrive(n("ap"), w * sides, [A(n("lp"), 0, 2 * sides)])
-        act(A("bn", 32, 64), ind(A("nst", 0, 8), A("off", 2, 4)), ACT.Identity, bias=kcol, scale=-0.5)
-        for b in range(4):
-            unpack(bank(1 + b, l1 - l0), b, A(n("lt"), l0, l1), A(n("ls"), l0, l1))
-            move = copy if b < 3 else actcopy
-            if left:
-                move(A(fh, PW * b, PW * b + BW), bank(1 + b, BW))
-            if right:
-                c0 = 512 * (1 + b) + (BW if left else 0)
-                move(A(fh, PW * b + BW + C, PW * b + FW), A("ps", c0, c0 + BW))
-        for k in others[::-1]:
-            act(A("bc", 32 * k, 32 * k + 32), zer, ACT.Identity, bias=A(n("lc"), col(k), col(k) + 1))
+        act(A("bn", 32, 64), ind(A(n("pw"), 0, 2), A("off", 2, 4)), ACT.Identity, bias=kcol, scale=-0.5)
+        borrowed(2, actcopy)
+        borrowed(3, actcopy)
+        landed = lambda k: spread(k, A(n("lc"), col(k), col(k) + 1))
+        order = others[::-1]
+        landed(order[0])
+        landed(order[1])
+        for j, k in enumerate(order):
+            if j + 2 < len(order):
+                landed(order[j + 2])
+            if j + 3 == len(order):
+                copy(A("bc", 256, 288), ind(A(n("lc"), 0, 11), A("off", 0, 2)))
             turn(A("aa", 32 * k, 32 * k + 32), A("bc", 32 * k, 32 * k + 32))
-        actcopy(A("bc", 256, 288), ind(A(n("lc"), 0, 11), A("off", 0, 2)))
         if t == 0:
             dma("sy", ap(A("vt", 0, 512)), T.v[:], [A("bc", 256, 288)], [A("vt", 0, 512)])
         for c in range(nc):
@@ -458,50 +481,55 @@ def rank_program(g, core, T, topo):
         pfw = A(n("pf"), 16 + s0, 16 + s1)
         lp = A(n("lp"), 0, 2 * sides)
         if left:
-            act(A("bn", 0, 32), ind(lp, A("off", 6, 8)), ACT.Identity, bias=float(-C))
+            act(A("bn", 0, 32), ind(lp, A("off", 2, 4)), ACT.Identity, bias=A("cf", 6, 7), scale=-0.5)
         if right:
-            act(A("bn", 64, 96), ind(lp, A("off", 8, 10) if left else A("off", 6, 8)), ACT.Identity, bias=float(C))
+            act(A("bn", 64, 96), ind(lp, A("off", 4, 6) if left else A("off", 2, 4)), ACT.Identity, bias=A("cf", 7, 8), scale=-0.5)
         turn(A("sd", 0, nr), A("bfl", 0, nr))
         sdw = A("sd", w0, w0 + ns)
         act(A("dr", 0, ns), sdw, ACT.Identity, bias=0.5, scale=0.5)
-        scan(A("zs", 0, w0 + ns), A("sd", 0, w0 + ns), A("dp", 0, w0 + ns), 16.0 * nb0, ALU.add, ALU.add)
         if base:
             comp("ve", lambda e: e.tensor_reduce(ap(A("tot", 0, 1)), ap(A("sd", 0, nr)), AxisListType.X, ALU.add), [A("sd", 0, nr)], [A("tot", 0, 1)])
         tot = A("tot", 0, 1) if base else 0.0
+        scan(A("zs", 0, w0 + ns), A("sd", 0, w0 + ns), A("dp", 0, w0 + ns), 16.0 * nb0, ALU.add, ALU.add)
         turn(A(n("pf"), 0, 96), A("bn", 0, 96))
+        zsw = A("zs", w0, w0 + ns)
+        if base:
+            ts(A("zt", 0, ns), zsw, tot, ALU.subtract)
+            zsw = A("zt", 0, ns)
         if t == R - 1:
             dma("sy", T.ol[:], T[n("pf")][0:128:16, 32:64], [A(n("pf"), 32, 64)], [])
         zw = A("zz", 0, ns)
-        tt(zw, A("zs", w0, w0 + ns), pfw, ALU.add)
+        tt(A("zi", 0, ns), zsw, pfw, ALU.add)
         scan(A("wp", 0, ns), A("rt", 0, ns), pfw, 0.0, ALU.add, ALU.min)
-        tt(A("hd", 0, ns), A("hc", 0, ns), pfw, ALU.subtract)
+        tt(zw, zsw, pfw, ALU.add)
+        ts(A("zb", 0, ns), A("zi", 0, ns), 15, ALU.bitwise_and)
         ts(A(n("voff"), 0, 3), A("wp", 15, ns, 16), float(BW), ALU.add, *((float(FW - 1), ALU.min) if right else (0.0, ALU.max)))
+        tt(A("hd", 0, ns), A("hc", 0, ns), pfw, ALU.subtract)
         for b in range(4):
             actcopy(A(n("vtl"), b, 4 * ns, 4), ind(A(fh, PW * b, PW * b + FW), A(n("voff"), 0, 3)))
         n4 = ns // 16
-        ts(A("zi", 0, ns), zw, tot, ALU.subtract)
-        scan(A("wz", 0, ns), A("rt", 0, ns), zw, 0.0, ALU.add, ALU.min)
         if base:
             act(A("ini", 1, 2), tot, ACT.Identity, bias=inic)
         if left:
             act(A("ini", 0, 1), A("zs", w0 - 1, w0), ACT.Identity, bias=A("ini", 1, 2) if base else inic, scale=-1.0)
         ini = A("ini", 0, 1) if left else inic
-        ts(A("zb", 0, ns), A("zi", 0, ns), 15, ALU.bitwise_and)
-        ts(A("wi", 0, n4), A("wz", 15, ns, 16), tot, ALU.subtract)
-        tt(A("dh", 0, ns), A("dr", 0, ns), A("hd", 0, ns), ALU.mult)
-        ts(A("e1", 0, ns), A("zb", 0, ns), icol, ALU.is_equal)
+        scan(A("wz", 0, ns), A("rt", 0, ns), zw, 0.0, ALU.add, ALU.min)
         ts(A("e2", 0, ns), A("zb", 0, ns), icol, ALU.is_lt)
-        ts(A("wa", 0, n4), A("wi", 0, n4), 4, ALU.arith_shift_right)
-        tt(A("x1", 0, ns), A("e1", 0, ns), A("dh", 0, ns), ALU.mult)
+        ts(A("e1", 0, ns), A("zb", 0, ns), icol, ALU.is_equal)
+        tt(A("dh", 0, ns), A("dr", 0, ns), A("hd", 0, ns), ALU.mult)
+        copy(A("wi", 0, n4), A("wz", 15, ns, 16))
         tt(A("x2", 0, ns), A("e2", 0, ns), sdw, ALU.mult)
+        tt(A("x1", 0, ns), A("e1", 0, ns), A("dh", 0, ns), ALU.mult)
+        ts(A("wa", 0, n4), A("wi", 0, n4), 4, ALU.arith_shift_right)
+        tt(A("x3", 0, ns), sdw, A("x2", 0, ns), ALU.subtract)
+        tt(A("vv", 0, ns), A("x1", 0, ns), A("x2", 0, ns), ALU.subtract)
         ts(A("so", 0, n4), A("wa", 0, n4), 5.0, ALU.mult, m4a, ALU.add)
+        ts(A("so", n4, 2 * n4), A("wa", 0, n4), 5.0, ALU.mult, m4b, ALU.add)
+        tt(A("vv", ns, 2 * ns), A("x1", 0, ns), A("x3", 0, ns), ALU.add)
         quant(A(n("qv"), 0, 128), A(n("sv"), 0, 128), A(n("vtl"), 0, 512))
         for b in range(4):
             layer(bank(1 + b, 128), b, A(n("qv"), 0, 128), A(n("sv"), 0, 128))
             act(A(fh, PW * b + FW, PW * b + PW), bank(1 + b, ns), ACT.Relu, scale=0.03125)
-        tt(A("vv", 0, ns), A("x1", 0, ns), A("x2", 0, ns), ALU.subtract)
-        ts(A("so", n4, 2 * n4), A("wa", 0, n4), 5.0, ALU.mult, m4b, ALU.add)
-        tt(A("vv", ns, 2 * ns), A("vv", 0, ns), sdw, ALU.add)
         copy(ind(A(n("win"), 0, 2 * WOFF), A("so", 0, 2 * n4)), A("vv", 0, 2 * ns))
         scan(A("sc", 0, nscan), A(n("win"), 0, nscan), A(n("win"), WOFF, WOFF + nscan), ini, ALU.add, ALU.subtract)
         copy(A(n("eoff"), 0, 28), A("sc", 5 * nb0 + 4, nscan, 5))

@@ -2,35 +2,50 @@ from concourse.bass import DstId, RemoteDMATransfer
 from concourse.mybir import dt, AluOpType, AxisListType, ActivationFunctionType
 
 N, C, S, L, R = 8, 448, 32, 14, 2
-HALF = C // 2
+PIECES = [(0, 128), (128, 320), (320, 448)]
 BW = 128
 FW = C + 2 * BW
-PW = FW + 48
-WOFF = 384
+NS = 48
+PW = FW + NS
+ROW = 48
+EB = 7 * ROW
+AT, AT2, VV = 0, 1, 1
+BLK = 129
+TAIL = ("g00 G02 g01 G03 g10 e0 G12 G13 p00 p01 p02 p03 g11 G22 e1 g20 R00 a00 w10 R01 a01 w11 u10 G23 g21 R02 a02 w12 u11 R03 a03 w13 u12 u13 e2 "
+        "R10 a10 w20 R11 a11 w21 u20 x0 R12 a12 w22 u21 R13 a13 w23 u22 u23 R20 a20 x1 R21 a21 R22 a22 R23 a23 x2")
+CUTS = [(0, 320), (320, 448)]
+FIRST = False
+EARLY = 6
+ORDER = True
+WLATE = True
+PAD = 16384.0
+TALL = 2.0 ** 20
 BIG = 1.0e29
 Q4, U8, BF, F32, I32, U16 = "float8_e4m3fn_x4", "uint8", "bfloat16", "float32", "int32", "uint16"
 
 SCRATCH = {"ps": ("psum", [128, 4096], F32)}
 for _n, _w, _d in [("xt", 4 * C, BF), ("ut", 512, BF), ("vt", 512, BF), ("uq", 128, Q4), ("us", 128, U8), ("uq2", 128, Q4),
                    ("us2", 128, U8), ("vq", 128, Q4), ("vs", 128, U8), ("wq", 512, Q4), ("wsc", 512, U8), ("eb", 1040, BF),
-                   ("eq", 512, Q4), ("es", 512, U8), ("one", 512, BF), ("idn", 128, BF), ("d0", 512, BF), ("junk", 512, BF),
-                   ("eqt", 512, BF), ("sct", 512, BF), ("off", 8, U16), ("uoff", 8, U16), ("so", 8, U16), ("pi", 8, I32),
-                   ("pj", 8, I32), ("zi", 64, I32), ("zb", 64, I32), ("wi", 4, I32), ("wa", 4, I32), ("t2", C, Q4), ("s2", C, U8)]:
+                   ("eq", 512, Q4), ("es", 512, U8), ("one", 512, BF), ("idn", 128, BF), ("d0", 5 * BLK + 1, BF),
+                   ("eqt", 5 * BLK + 1, BF), ("sct", 5 * BLK + 1, BF),
+                   ("off", 24, U16), ("uoff", 8, U16), ("so", 4, U16), ("eo", 4, U16), ("pi", 8, I32),
+                   ("pj", 8, I32), ("pl", 8, I32), ("wi", 4, I32), ("wa", 4, I32), ("we", 4, I32), ("t2", C, Q4), ("s2", C, U8),
+                   ("vtl", 512, BF)]:
     SCRATCH[_n] = ("sbuf", [128, _w], _d)
-for _w, _ns in [(4, "pp fl tot ini"), (8, "pk fo cf"), (16, "pc nst"), (32, "zer neg"), (48, "g1 g2 df u1 u2 u3 th2"),
-                (64, "zz zt rt rt0 hc wp hd dr dh e1 e2 x1 x2 x3 wz"), (96, "bn"), (112, "io16 thc tx ty tz th"), (128, "junk2 vv"),
-                (160, "bfl sd dp zs"), (256, "aa"), (288, "bc"), (WOFF, "sc"), (416, "om d1"), (C, "et ys"), (8 * HALF, "rl")]:
+for _w, _ns in [(4, "ini wp ta tb tc"), (8, "pk ms0 hh cc"), (16, "pc nst cm cf lt16 hf"), (32, "bn tab1 tab2"),
+                (48, "mk ha hb vv1 vv2 rr"), (64, "rt bc aa"), (96, "pf df"), (112, "io16 thc tx ty tz th u1 u2 u3 th2"),
+                (160, "bfl junk2"), (208, "sd zs"), (320, "sc"), (C, "ys"), (PW, "iof"), (4 * C, "rl"),
+                (EB + 32 * ROW, "om")]:
     for _n in _ns.split():
         SCRATCH[_n] = ("sbuf", [128, _w], F32)
 for _t in range(R):
-    for _n, _w, _d in [("t", C, Q4), ("s", C, U8), ("lt", 2 * BW, Q4), ("ls", 2 * BW, U8), ("fh", 4 * PW, BF), ("pm", 16, F32),
-                       ("lc", 16, F32), ("lp", 4, F32), ("pf", 96, F32), ("pw", 16, F32), ("voff", 4, U16), ("vtl", 512, BF),
-                       ("qv", 128, Q4), ("sv", 128, U8), ("win", 2 * WOFF, F32), ("eoff", 28, U16), ("etl", 4 * C, BF),
+    for _n, _w, _d in [("t", C, Q4), ("s", C, U8), ("lt", 2 * BW, Q4), ("ls", 2 * BW, U8), ("fh", 4 * PW, BF),
+                       ("lc", 16, F32), ("lp", 12, F32), ("wps", 64, F32), ("voff", 4, U16),
+                       ("qv", 128, Q4), ("sv", 128, U8), ("win", 320, F32), ("wim", 320, F32), ("eoff", 28, U16), ("etl", 4 * C, BF),
                        ("qe", C, Q4), ("se", C, U8), ("xn", 4 * C, BF)]:
         SCRATCH[_n + str(_t)] = ("sbuf", [128, _w], _d)
 
-SEMAPHORES = (["pe", "ve", "se", "ge"] + ["d%d" % i for i in range(32)] + [a + str(t) for t in range(R) for a in ("at", "ap")]
-              + ["ac%d_%d" % (t, k) for t in range(R) for k in range(N)])
+SEMAPHORES = (["pe", "ve", "se", "ge"] + ["d%d" % i for i in range(40)] + [a + str(t) for t in range(R) for a in ("at", "ap", "ac")])
 
 
 def A(name, c0, c1, step=1, p0=0, p1=128):
@@ -57,7 +72,7 @@ def emit(g, T, ops):
     lane = [o[0] if o[1] == "c" else ("x", i) for i, o in enumerate(ops)]
     known = {q: {} for q in queues}
     clock, waits, wanted = [None] * n, [[] for _ in ops], set()
-    by = {}
+    by, across = {}, []
     for i, (q, kind, call, rd, wr) in enumerate(ops):
         if kind == "a":
             clock[i] = {lane[i]: i}
@@ -70,6 +85,9 @@ def emit(g, T, ops):
                         continue
                     if (is_w or o_w or ps) and _meet(mine, other):
                         deps.add(j)
+            if q == "ve":
+                deps.update(across)
+                across = [i] if len(set(a[1] // 32 for a in rd)) > 1 else []
             k = known[q]
             for j in sorted(deps, reverse=True):
                 if k.get(lane[j], -1) < j:
@@ -84,11 +102,6 @@ def emit(g, T, ops):
             by.setdefault(a[0], []).append((i, a, False))
         for a in wr:
             by.setdefault(a[0], []).append((i, a, True))
-    last = {}
-    for i, o in enumerate(ops):
-        if o[1] == "c":
-            last[o[0]] = i
-    wanted.update(last.values())
     mark, count, nd = {}, {q: 0 for q in queues}, 0
     for i, (q, kind, call, rd, wr) in enumerate(ops):
         if kind == "c" and i in wanted:
@@ -111,7 +124,7 @@ def emit(g, T, ops):
         else:
             call[0](queues[q], T.sem[mark[i][0]])
     for i, o in enumerate(ops):
-        if o[1] != "c" or last[o[0]] == i:
+        if o[1] != "c" and i not in wanted:
             g.wait_ge(T.sem[mark[i][0]], mark[i][1])
 
 
@@ -139,6 +152,9 @@ def rank_program(g, core, T, topo):
     def ind(win, off):
         return ("@", win, off)
 
+    def part(a, p0, p1):
+        return (a[0], p0, p1) + a[3:]
+
     def comp(q, call, rd, wr):
         ops.append([q, "c", call, rd, wr])
 
@@ -162,6 +178,9 @@ def rank_program(g, core, T, topo):
 
     def scan(o, a, b, init, op0, op1):
         comp("ve", lambda e: e.tensor_tensor_scan(ap(o), ap(a), ap(b), ap(init), op0, op1), regs(a, b, init), [o])
+
+    def least(o, i):
+        comp("ve", lambda e: e.tensor_reduce(ap(o), ap(i), AxisListType.X, ALU.min), [i], [o])
 
     def turn(o, i):
         comp("ve", lambda e: e.transpose(ap(o), ap(i)), [i], [o])
@@ -223,86 +242,141 @@ def rank_program(g, core, T, topo):
 
     left, right = r > 0, r < N - 1
     sides = int(left) + int(right)
-    base = 0 if r < N // 2 else N // 2
-    extra = {N // 2 - 1: N // 2, N // 2: N // 2 - 1}.get(r)
-    nc = 1 if extra is None else 2
-    ranks = list(range(0, r + 2)) if r < N // 2 else list(range(r - 1, N))
-    nr = 32 * len(ranks)
-    ns = 48
-    back = -(-S * r // (L + 1)) if r <= N // 2 else -(-S * (N - r) // (L - 1))
-    s0 = 16 - back if right else 0
-    s1 = s0 + ns
-    w0 = 32 * ranks.index(r) - 16 + s0
-    nb0 = (L * (16 - s0) + min(128, 32 * r) + 15) // 16 if left else 1
-    nscan = 5 * (nb0 + 28)
-    col = lambda k, at=r: 0 if k == at else 4 + k - int(k > at)
-    kcol, m4b, inic = [A("cf", j, j + 1) for j in range(3)]
-    icol, m4a = A("pk", 0, 1), A("pk", 2, 3)
-    zer = A("zer", 0, 32)
+    low_half = r < N // 2
+    back_of = lambda k: -(-S * (N // 2 - 1) // (L + 1)) if k < N // 2 else -(-S * (N // 2) // (L + 1))
+    back = back_of(r)
+    ranks = list(range(0, min(r + 2, N))) if low_half else list(range(r - 1, N))
+    nk = len(ranks)
+    nr = S * nk
+    early = nk >= EARLY
+    w0 = 16 + S * ranks.index(r) - back
+    k0 = S * r - back
+    reach = lambda k: max(0, min(N * S // 2, k + 1, N * S - 1 - k))
+    nb = -(-(L * back + reach(k0)) // 16) + 1
+    nscan = 5 * (nb + 27)
+    z0 = w0 if (r == 0 or not low_half) else 16
+    zl = 16 + nr + (0 if right else 16 - back)
+    z1 = w0 + NS if low_half else zl + 1
+    col = lambda k, at=r: 3 + (k - at) % N
+    icol, kcol, m4, quad, quad2 = [A("pk", j, j + 1) for j in range(5)]
+    cf = lambda j: A("cf", j, j + 1)
+    kc2, mx, vcol, zinit, inic, scol = [cf(j) for j in range(6)]
+    off_pair, off_rank, off_spread = A("off", 0, 2), A("off", 2, 6), A("off", 6, 6 + 2 * nk)
 
-    cuts = [(0, BW), (C - BW, C), (BW, C - BW)]
-    for j, (a, b) in enumerate(cuts):
-        dma("se" if j == 1 else "sy", ap(A("xt", 4 * a, 4 * b)), T.x[:, 4 * a:4 * b], [], [A("xt", 4 * a, 4 * b)])
+    cuts = CUTS
     dma("se", ap(A("ut", 0, 512)), T.u[:], [], [A("ut", 0, 512)])
-    dma("sy", b8(A("wq", 0, 512)), T.wc[:], [A("xt", 0, 4 * C), A("ut", 0, 512)], [A("wq", 0, 512)])
-    dma("sy", ap(A("wsc", 0, 512)), T.ws[:], [], [A("wsc", 0, 512)])
+    for j, (a, b) in enumerate(cuts):
+        dma("sy", ap(A("xt", 4 * a, 4 * b)), T.x[:, 4 * a:4 * b], [], [A("xt", 4 * a, 4 * b)])
+
+    def load_w(after):
+        dma("sy", b8(A("wq", 0, 512)), T.wc[:], after, [A("wq", 0, 512)])
+        dma("sy", ap(A("wsc", 0, 512)), T.ws[:], [], [A("wsc", 0, 512)])
+    if not WLATE:
+        load_w([A("xt", 0, 4 * C), A("ut", 0, 512)])
 
     comp("ge", lambda e: e.iota(ap(A("pi", 0, 8)), [[0, 8]], 0, 1), [], [A("pi", 0, 8)])
-    memset(A("one", 0, 512), 1.0)
+    memset(A("one", 0, 128), 1.0)
     memset(A("eb", 0, 1040), 0.0)
     comp("ge", lambda e: e.affine_select(ap(A("idn", 0, 128)), ap(A("one", 0, 128)), [[-1, 128]], ALU.is_equal, 0.0, 0, 1),
          [A("one", 0, 128)], [A("idn", 0, 128)])
     iota(A("io16", 0, 112), [[0, 7], [1, 16]], 0)
-    iota(A("hc", 0, 64), [[1, 64]], FW - BW - 1)
-    iota(A("fo", 2, 6), [[1, 4]], 0)
+    iota(A("hf", 0, 16), [[1, 8], [0, 2]], 0)
+    iota(A("iof", 0, PW), [[1, PW]], 0)
+    io = lambda a, b: A("io16", a, b)
+    ts(A("pl", 0, 1), A("pi", 0, 1), 15, ALU.bitwise_and)
+    ts(A("pl", 1, 2), A("pi", 0, 1), 31, ALU.bitwise_and)
+    ts(A("pl", 2, 3), A("pi", 0, 1), 3, ALU.bitwise_and)
+    ts(A("pl", 3, 4), A("pi", 0, 1), 5, ALU.arith_shift_right)
+    ts(A("pl", 4, 5), A("pi", 0, 1), 4, ALU.arith_shift_right, 6, ALU.bitwise_and)
     ts(A("pj", 0, 8), A("pi", 0, 8), 7, ALU.bitwise_and)
-    memset(A("d0", 0, 512), 1.0)
-    ts(A("uoff", 0, 8), A("pj", 0, 8), 16.0, ALU.mult)
-    ts(A("pj", 0, 1), A("pi", 0, 1), 15, ALU.bitwise_and)
-    ts(A("pj", 1, 2), A("pi", 0, 1), 31, ALU.bitwise_and)
-    ts(A("pj", 2, 3), A("pi", 0, 1), 3, ALU.bitwise_and)
-    copy(A("pk", 0, 3), A("pj", 0, 3))
+    copy(A("pk", 0, 5), A("pl", 0, 5))
+    ts(A("ms0", 4, 8), A("pj", 4, 8), -1.0, ALU.mult, 7.0, ALU.add)
+    ts(A("uoff", 0, 4), A("pj", 0, 4), 16.0, ALU.mult)
+    ts(mx, icol, float(back), ALU.is_ge, PAD, ALU.mult)
+    tt(A("ms0", 0, 4), A("ms0", 4, 8), A("pj", 4, 8), ALU.max)
+    ts(A("rt", 0, 64), io(0, 64), icol, ALU.is_equal, TALL, ALU.mult)
+    ts(A("lt16", 0, 16), io(0, 16), icol, ALU.is_lt)
+    ts(A("uoff", 4, 8), A("ms0", 0, 4), 16.0, ALU.mult)
+    memset(A("d0", 0, nk * BLK), 1.0)
+    memset(A("om", EB, EB + 8 * ROW, 3), BIG)
+    memset(A("om", EB + 1, EB + 8 * ROW, 3), 0.0)
+    for c0 in (2, ROW - 3, ROW - 1):
+        memset(A("om", c0, EB + 8 * ROW, ROW), BIG)
     actcopy(A("eb", 2, 514, 4), A("idn", 0, 128))
     actcopy(A("eb", 523, 1035, 4), A("idn", 0, 128))
-    for b in range(4):
-        c0 = 520 * (b % 2) + 2 - 2 * (b // 2)
-        quant(A("eq", 128 * b, 128 * b + 128), A("es", 128 * b, 128 * b + 128), A("eb", c0, c0 + 512))
-    fill(A("om", 0, 416, 2), 0.0)
-    fill(A("d1", 0, 256, 2), 0.0)
-    fill(A("om", 1, 416, 32), BIG)
-    fill(A("om", 31, 416, 32), BIG)
-    memset(A("neg", 0, 32), -1.0)
-    memset(A("dp", 0, 160), 0.0)
-    memset(A("bn", 0, 96), 0.0)
-    for a, b in cuts[:2]:
-        quant(A("t0", a, b), A("s0", a, b), A("xt", 4 * a, 4 * b))
     quant(A("uq", 0, 128), A("us", 0, 128), A("ut", 0, 512))
     comp("ve", lambda e: e.tensor_copy(ap(A("uq2", 0, 128)).bitcast(dt.uint32), ap(A("uq", 0, 128)).bitcast(dt.uint32).indirect(ap(A("uoff", 0, 8)))),
          [A("uq", 0, 128), A("uoff", 0, 8)], [A("uq2", 0, 128)])
-    quant(A("t0", BW, C - BW), A("s0", BW, C - BW), A("xt", 4 * BW, 4 * (C - BW)))
-    act(A("thc", 0, 96), A("io16", 0, 96), ACT.Identity, bias=-8.0)
-    act(A("thc", 96, 112), A("io16", 96, 112), ACT.Identity, bias=-1.5)
-    act(A("cf", 5, 6), icol, ACT.Identity, scale=-1.0)
-    act(kcol, A("pk", 1, 2), ACT.Identity, bias=6.5, scale=float(L))
-    act(m4b, m4a, ACT.Identity, bias=float(WOFF + 5))
-    act(inic, icol, ACT.Identity, bias=float(BW - 16 - (0 if left else 16 * nb0)))
-    act(A("rt0", 0, 64), A("io16", 0, 64), ACT.Abs, bias=A("cf", 5, 6))
-    act(A("cf", 6, 7), A("pk", 1, 2), ACT.Identity, bias=6.5 - C, scale=float(L))
-    act(A("cf", 7, 8), A("pk", 1, 2), ACT.Identity, bias=6.5 + C, scale=float(L))
-    act(A("rt", 0, 64), A("rt0", 0, 64), ACT.Relu, bias=1.0e6, scale=-1.0e6)
-    fill(A("fo", 1, 2), col(base if extra is None else extra))
-    fill(zer, 0.0)
-    act(A("d0", 32 * base, 32 * base + 128), A("idn", 0, 128), ACT.Identity, bias=1.0, scale=-2.0)
-    if extra is not None:
-        for a in range(4):
-            act(A("d0", 256 + 32 * extra, 288 + 32 * extra, 1, 32 * a, 32 * a + 32), A("idn", 32 * a, 32 * a + 32, 1, 32 * a, 32 * a + 32),
-                ACT.Identity, bias=1.0, scale=-2.0)
     actcopy(A("us2", 0, 128), ind(A("us", 0, 128), A("uoff", 0, 8)))
-    for a in range(4):
-        fill(A("fo", 0, 1, 1, 32 * a, 32 * a + 32), col(base + a))
+    for a, b in cuts:
+        quant(A("t0", a, b), A("s0", a, b), A("xt", 4 * a, 4 * b))
+    for b in range(4):
+        c0 = 520 * (b % 2) + 2 - 2 * (b // 2)
+        quant(A("eq", 128 * b, 128 * b + 128), A("es", 128 * b, 128 * b + 128), A("eb", c0, c0 + 512))
+
+    act(A("thc", 16, 112), io(16, 112), ACT.Identity, bias=-8.0)
+    act(A("thc", 0, 16), io(0, 16), ACT.Identity, bias=-1.5)
+    first, ops = ops, []
+    act(kc2, kcol, ACT.Identity, bias=13.0 + 2 * C * r, scale=2.0 * L)
+    act(vcol, mx, ACT.Identity, bias=2.0 * (BW - C * r), scale=-1.0)
+    act(zinit, mx, ACT.Identity, bias=32.0 * nb - 2 * C * r + 0.5 + (0 if left else 2 * back), scale=-1.0)
+    act(scol, A("rt", 15, 16), ACT.Identity, bias=-2.0, scale=2.5 / TALL)
+    act(A("ha", 0, NS), A("rt", 16, 64), ACT.Identity, bias=1.0, scale=-1.0 / TALL)
+    act(A("hb", 0, NS), A("rt", 15, 63), ACT.Identity, scale=1.25 / TALL)
+    act(inic, vcol, ACT.Identity, bias=icol, scale=0.5) if left else act(inic, icol, ACT.Identity, bias=float(BW - 16 * nb - back))
+    act(A("tab1", 0, 32, 2), A("lt16", 0, 16), ACT.Identity, scale=-1.0)
+    act(A("tab2", 0, 32, 2), A("lt16", 0, 16), ACT.Identity, bias=1.0, scale=-1.0)
+    for j, k in enumerate(ranks):
+        a = k // 2
+        c0 = BLK * j + 32 * (k % 2)
+        act(A("d0", c0, c0 + 32, 1, 32 * a, 32 * a + 32), A("idn", 32 * a, 32 * a + 32, 1, 32 * a, 32 * a + 32), ACT.Identity, bias=1.0, scale=-1.0)
+    fill(A("d0", 0, nk * BLK, BLK), 0.0)
+    fill(A("d0", BLK - 1, nk * BLK, BLK), -1.0)
+    fill(A("eqt", BLK - 1, nk * BLK, BLK, 32, 64), 64.0)
+    fill(A("eqt", BLK - 1, nk * BLK, BLK, 64, 128), 64.0)
+    fill(A("eqt", BLK - 1, nk * BLK, BLK, 0, 32), 65.0)
     for t in range(R):
-        fill(A("vtl%d" % t, 4 * ns, 512), 0.0)
-        fill(A("lc%d" % t, 1, 4), 0.0)
+        actcopy(A("lp%d" % t, 4, 5), mx)
+    fill(A("nst", 0, 4, 1, 64, 128), 0.0)
+    fill(A("pf", 0, 16), 0.0)
+    fill(A("pf", 48, 96), PAD)
+    fill(A("sd", 0, 16), -1.0)
+    fill(A("sd", 16 + nr, 16 + nr + 16), -1.0)
+    if sides == 1:
+        act(cf(12), icol, ACT.Identity, bias=L - 2.0 * L * back + (2 * C * N if left else 0), scale=2.0 * L)
+    if not low_half:
+        act(A("sd", zl, zl + 1), zinit, ACT.Identity, bias=0.0 if right else 16.0 - back, scale=-0.5)
+
+    def clear(t):
+        act(A("win%d" % t, 0, nscan + 5), A("iof", 0, nscan + 5), ACT.Identity, scale=0.0)
+        act(A("wim%d" % t, 0, nscan), A("iof", 0, nscan), ACT.Identity, scale=0.0)
+        fill(A("win%d" % t, 4, nscan + 5, 5), -16.0)
+    later, ops = ops, []
+    memset(A("vtl", 4 * NS, 512), 0.0)
+    ts(A("wi", 0, 4), A("hf", 0, 4), quad2, ALU.add, float(N - r), ALU.add)
+    ts(off_pair, io(0, 2), quad2, ALU.add)
+    ts(A("wa", 0, 4), A("wi", 0, 4), N - 1, ALU.bitwise_and)
+    copy(off_spread, A("hf", 0, 2 * nk))
+    ts(off_rank, A("wa", 0, 4), 3.0, ALU.add)
+    ts(A("d0", 64, nk * BLK, BLK), A("hf", ranks[0], ranks[0] + nk), quad, ALU.is_le)
+    tt(A("tab1", 1, 32, 2), A("lt16", 0, 16), A("rt", 0, 16), ALU.subtract)
+    for t in range(R):
+        memset(A("lc%d" % t, 0, 3), 0.0)
+    ts(A("tab2", 1, 32, 2), A("tab1", 1, 32, 2), -1.0, ALU.add)
+    if sides == 1:
+        ts(cf(13), icol, float(back), ALU.is_ge if left else ALU.is_lt)
+    spare, ops = ops, []
+    tt(A("mk", 0, NS), A("ha", 0, NS), A("hb", 0, NS), ALU.subtract)
+    for t in range(R):
+        if not left:
+            ts(A("lp%d" % t, 0, 1), cf(12), cf(13), ALU.mult, mx, ALU.add)
+        if not right:
+            ts(A("lp%d" % t, 8, 9), cf(12), cf(13), ALU.mult)
+    last, ops = ops, first
+
+    def gap(cnt=1):
+        ops.extend(spare[:cnt])
+        del spare[:cnt]
 
     for t in range(R):
         n = lambda s: s + str(t)
@@ -318,258 +392,244 @@ def rank_program(g, core, T, topo):
         send_sides(n("at"), psc)
         l0, l1 = (0 if left else BW), (2 * BW if right else BW)
         arrive(n("at"), 2 * w * sides, [A(n("lt"), l0, l1), A(n("ls"), l0, l1)])
-        mm(bank(0, C), A("uq2", 0, 128), A("us2", 0, 128), A(tq, 0, C), A(tsc, 0, C))
+        cut = PIECES[-1][0] if t else cuts[-1][0]
+        for h, (c0, c1) in enumerate([(0, cut), (cut, C)]):
+            mm(bank(4 + h, c1 - c0), A("uq2", 0, 128), A("us2", 0, 128), A(tq, c0, c1), A(tsc, c0, c1))
+            act(A("ys", c0, c1), bank(4 + h, c1 - c0), ACT.Abs)
         for b in range(4):
-            unpack(bank(1 + b, C), b, A(tq, 0, C), A(tsc, 0, C))
+            unpack(bank(b, C), b, A(tq, 0, C), A(tsc, 0, C))
         if t == R - 1:
             quant(A("vq", 0, 128), A("vs", 0, 128), A("vt", 0, 512))
+        else:
+            gap(2)
         for l in range(L):
-            turn(A("et", 32 * l, 32 * l + 32), A("ps", l, C, L))
-        fown = lambda b: actcopy(A(fh, PW * b + BW, PW * b + BW + C), bank(1 + b, C))
-        fown(0)
-        m = lambda a, b: A("om", 2 * a + 1, 2 * b + 1, 2)
-        low = lambda a, b: A("d1", 2 * a, 2 * b, 2)
-        e_to = lambda row, k: act(A("d1", 32 * row + 1, 32 * row + 28, 2), A("et", k, C, 32), ACT.Abs)
-        pair = lambda row, frm: tt(low(16 * row, 16 * row + 15), m(16 * frm, 16 * frm + 15), m(16 * frm + 1, 16 * frm + 16), ALU.min)
-        wipe = lambda row: memset(A("om", 32 * row + 2, 32 * row + 30, 2), 0.0)
-        step = lambda row, frm: scan(A("om", 32 * row + 2, 32 * row + 30), A("om", 32 * frm + 4, 32 * frm + 32), A("d1", 32 * row, 32 * row + 28),
-                                     0.0, ALU.min, ALU.max)
-        act(m(1, 15), A("et", 0, C, 32), ACT.Abs)
-        act(m(129, 143), A("et", 7, C, 32), ACT.Abs)
-        for row, k in ((1, 1), (9, 6), (2, 2), (10, 5), (3, 3), (11, 4), (4, 4), (5, 5), (6, 6), (7, 7)):
-            e_to(row, k)
-        for b in range(1, 4):
+            turn(A("om", EB + 3 * l + 5, EB + 32 * ROW, ROW), A("ys", l, C, L))
+        fown = lambda b: actcopy(A(fh, PW * b + BW, PW * b + BW + C), bank(b, C))
+        om = lambda a, cnt, st=3: A("om", a, a + st * (cnt - 1) + 1, st)
+        o_ = lambda k: EB - ROW * k
+        pair = lambda k: tt(om(o_(k) + 7, 15), om(o_(k) + 2, 15), om(o_(k) + 5, 15), ALU.min)
+
+        def step(k, p0=0, p1=128, q0=None):
+            q0 = p0 if q0 is None else q0
+            scan(part(om(o_(k) + 3, 42, 1), p0, p1), part(om(o_(k - 1) + 6, 42, 1), q0, q0 + p1 - p0), part(om(EB + ROW * k + 3, 42, 1), p0, p1),
+                 0.0, ALU.min, ALU.max)
+        for b in range(4):
             fown(b)
-        fill(A(n("win"), 0, nscan), 0.0)
-        fill(A(n("win"), WOFF, WOFF + nscan), 0.0)
-        fill(A(n("win"), 4, nscan, 5), 16.0)
+        if t == 0:
+            ops.extend(later)
+        gap(2)
         for k in range(1, 4):
-            pair(k, k - 1)
-            if k > 1:
-                wipe(k - 1)
-            pair(8 + k, 7 + k)
-            if k > 1:
-                wipe(7 + k)
-            step(k, k - 1)
-            step(8 + k, 7 + k)
-        pair(12, 3)
-        wipe(3)
-        copy(A("d1", 32 * 12 + 1, 32 * 12 + 28, 2), m(177, 191))
-        pair(4, 3)
-        step(12, 3)
-        step(4, 3)
-        scan(A(n("pm"), 0, L), m(193, 207), m(193, 207), BIG, ALU.min, ALU.min)
-        cost = A(n("pm"), L - 1, L)
-        others = [(r + d) % N for d in range(1, N)]
+            pair(k - 1)
+            gap(2)
+            step(k)
+            gap(2)
+        pair(3)
+        gap(2)
+        lo3 = om(o_(3) + 10, 13)
+        cost = A(n("lc"), 3, 4)
+        step(4)
+        tt(A("cm", 0, 13, 1, 0, 64), part(lo3, 0, 64), part(lo3, 64, 128), ALU.max)
+        least(part(cost, 0, 64), A("cm", 0, 13, 1, 0, 64))
+        least(part(cost, 64, 128), A("cm", 0, 13, 1, 0, 64))
+        others = sorted(set(range(N)) - {r}, key=lambda k: (abs(2 * k - N + 1), (k - r) % N)) if ORDER else [(r + d) % N for d in range(1, N)]
         full, wf = masks(others[0], 1)
 
         def send_costs(e, s, t=t, cost=cost, full=full, others=others):
-            e.remote_dma_fused([RemoteDMATransfer(dst_ids=[dst(k) for k in others], dma_engine_mask=full[0], remote_sem=T.sem["ac%d_%d" % (t, r)],
+            e.remote_dma_fused([RemoteDMATransfer(dst_ids=[dst(k) for k in others], dma_engine_mask=full[0], remote_sem=T.sem["ac%d" % t],
                                                   srcs=[ap(cost)], dsts=[ap(A("lc%d" % t, col(r, k), col(r, k) + 1)) for k in others])], local_sem=s)
         ops.append(["ge", "d", (send_costs, wf), [cost], []])
-        for k in others:
-            arrive("ac%d_%d" % (t, k), wf, [A(n("lc"), col(k), col(k) + 1)])
-        actcopy(A(n("lc"), 0, 1), cost)
+        arrive("ac%d" % t, wf * (N - 1), [A(n("lc"), 4, 3 + N)])
 
         def borrowed(b, move):
-            unpack(bank(1 + b, l1 - l0), b, A(n("lt"), l0, l1), A(n("ls"), l0, l1))
+            unpack(bank(b, l1 - l0), b, A(n("lt"), l0, l1), A(n("ls"), l0, l1))
             if left:
-                move(A(fh, PW * b, PW * b + BW), bank(1 + b, BW))
+                move(A(fh, PW * b, PW * b + BW), bank(b, BW))
             if right:
-                c0 = 512 * (1 + b) + (BW if left else 0)
+                c0 = 512 * b + (BW if left else 0)
                 move(A(fh, PW * b + BW + C, PW * b + FW), A("ps", c0, c0 + BW))
-        tx = lambda a, b: tt(A("tx", a, b), m(a, b), low(a + 17, b + 17), ALU.is_le)
-        ty = lambda a, b: tt(A("ty", a, b), low(a + 15, b + 15), m(a + 1, b + 1), ALU.is_le)
+            if sides == 1:
+                c0 = PW * b + (BW + C if left else 0)
+                fill(A(fh, c0, c0 + BW), 0.0)
+        o6 = o_(6)
+        tx = lambda a, b: tt(A("tx", a, b), om(o6 + 3 * a + 2, b - a), om(o6 + 3 * a + 10, b - a), ALU.is_le)
+        ty = lambda a, b: tt(A("ty", a, b), om(o6 + 3 * a + 4, b - a), om(o6 + 3 * a + 5, b - a), ALU.is_le)
         tz = lambda a, b: tt(A("tz", a, b), A("tx", a, b), A("thc", a, b), ALU.add)
         th = lambda a, b: tt(A("th", a, b), A("tz", a, b), A("ty", a, b), ALU.add)
-        two = lambda o, a, b, op: tt(A(o, 1, 46), A(a[0], 1 + a[1], 46 + a[1]), A(b[0], 1 + b[1], 46 + b[1]), op)
-        if t == 0:
-            copy(A("off", 0, 6), A("fo", 0, 6))
-        for k, gap in ((5, (tx, ty)), (6, (tz, th))):
-            pair(k, k - 1)
-            wipe(k - 1)
-            gap[0](1, 63)
-            step(k, k - 1)
-            gap[1](1, 63)
-        pair(7, 6)
-        wipe(6)
-        two("g1", ("tx", 0), ("ty", 0), ALU.max)
-        step(7, 6)
-        tx(65, 110)
-        ty(65, 110)
-        scan(A("pc", 0, L), m(113, 127), m(113, 127), BIG, ALU.min, ALU.min)
-        tz(65, 110)
-        act(A("junk2", 0, L), A("pc", 0, L), ACT.Sign, bias=cost, scale=-1.0, acc=A("nst", 8, 9))
-        two("g2", ("tx", 0), ("ty", 0), ALU.min)
-        th(65, 110)
-        tt(A("df", 1, 47), A("th", 17, 63), A("th", 16, 62), ALU.subtract)
-        spread = lambda k, c: ts(A("bc", 32 * k, 32 * k + 32), zer, c, ALU.add)
-        spread(r, cost)
-        two("u1", ("g1", 0), ("df", 0), ALU.mult)
-        two("u2", ("g2", 0), ("df", 1), ALU.mult)
-        turn(A("aa", 32 * r, 32 * r + 32), A("bc", 32 * r, 32 * r + 32))
-        two("u3", ("u1", 0), ("th", 15), ALU.add)
-        two("th2", ("u3", 0), ("u2", 0), ALU.add)
-        borrowed(0, copy)
-        borrowed(1, copy)
-        if sides == 1:
-            for b in range(4):
-                c0 = PW * b + (0 if not left else BW + C)
-                memset(A(fh, c0, c0 + BW), 0.0)
-        pw = lambda q, c0, c1: A(n("pw"), c0, c1, 1, 32 * q, 32 * q + 32)
-        nst = lambda c0, c1, q=None: A("nst", c0, c1) if q is None else A("nst", c0, c1, 1, 32 * q, 32 * q + 32)
+        two = lambda o, a, b, op, c0, c1: tt(A(o, c0, c1), A(a[0], c0 + a[1], c1 + a[1]), A(b[0], c0 + b[1], c1 + b[1]), op)
+        df = lambda c0, c1: two("df", ("th", 1), ("th", 0), ALU.subtract, c0, c1)
+        u1 = lambda c0, c1: two("u1", ("ty", 0), ("df", -17), ALU.mult, c0, c1)
+        u2 = lambda c0, c1: two("u2", ("tx", 0), ("df", -16), ALU.mult, c0, c1)
+        u3 = lambda c0, c1: two("u3", ("u1", 0), ("th", -17), ALU.add, c0, c1)
+        th2 = lambda c0, c1: two("th2", ("u3", 0), ("u2", 0), ALU.add, c0, c1)
+        spread = lambda: copy(A("bc", 0, 64), ind(A(n("lc"), 0, 3 + N), off_rank))
+        pair(4)
+        tx(48, 111)
+        ty(48, 111)
+        step(5)
+        tz(48, 111)
+        pair(5)
+        th(48, 111)
+        step(6)
+        tx(16, 47)
+        ty(16, 47)
+        df(48, 94)
+        pair(6)
+        tz(16, 47)
+        u1(65, 110)
+        step(7)
+        tx(1, 14)
+        th(16, 47)
+        ty(1, 14)
+        scan(A("pc", 0, L), om(5, L), om(5, L), BIG, ALU.min, ALU.min)
+        tz(1, 14)
+        df(16, 30)
+        u2(65, 110)
+        u3(65, 110)
+        th(1, 14)
+        u1(33, 46)
+        u2(33, 46)
+        th2(65, 110)
+        u3(33, 46)
+        gap(len(spare))
+        if FIRST:
+            spread()
+        th2(33, 46)
+        if not FIRST:
+            spread()
+        nst = lambda k, k1=None: A("nst", k, k1 or k + 1, 1, 0, 64)
+        act(A("junk2", 0, L, 1, 0, 64), A("pc", 0, L, 1, 0, 64), ACT.Sign, bias=part(cost, 0, 64), scale=-1.0, acc=nst(8))
 
-        def back_to(k, frm, name, o, acc, p1=128):
-            act(A("junk2", 16 * k + 16, 16 * k + 29, 1, 0, p1), A(name, o + 1, o + L, 1, 0, p1), ACT.Sign, bias=A("nst", frm, frm + 1, 1, 0, p1),
-                scale=1.0 if frm == 8 else 2.0, acc=acc)
-        back_to(6, 8, "th", 96, nst(6, 7))
-        act(pw(3, 1, 2), nst(8, 9, 3), ACT.Identity, bias=13.0, scale=2.0)
-        back_to(5, 6, "th", 80, nst(5, 6))
-        actcopy(pw(3, 0, 1), nst(6, 7, 3))
-        back_to(4, 5, "th", 64, nst(4, 5))
-        back_to(2, 4, "th2", 32, nst(2, 3))
-        back_to(3, 4, "th", 48, nst(3, 4))
-        actcopy(pw(2, 0, 2), nst(4, 6, 2))
-        back_to(0, 2, "th2", 0, pw(0, 0, 1), 32)
-        back_to(1, 2, "th", 16, pw(0, 1, 2), 32)
-        actcopy(pw(1, 0, 2), nst(2, 4, 1))
+        def back_to(k, frm, name):
+            o = 16 * (6 - k)
+            act(A("junk2", 16 * k + 16, 16 * k + 29, 1, 0, 64), A(name, o + 1, o + L, 1, 0, 64), ACT.Sign, bias=nst(frm),
+                scale=1.0 if frm == 8 else 2.0, acc=nst(k))
+        lc = lambda k: A(n("lc"), col(k), col(k) + 1)
+        if WLATE and t == 0:
+            load_w([nst(8)])
+        back_to(6, 8, "th")
+        act(nst(7), nst(8), ACT.Identity, bias=13.0, scale=2.0)
+        back_to(4, 6, "th2")
+        back_to(5, 6, "th")
+        back_to(2, 4, "th2")
+        back_to(3, 4, "th")
+        actcopy(part(nst(4, 8), 64, 128), nst(4, 8))
+        back_to(0, 2, "th2")
+        back_to(1, 2, "th")
+        act(A("bn", 0, 32), ind(A("nst", 0, 8), off_pair), ACT.Identity, bias=kc2, scale=-1.0)
+        for b in range(4):
+            borrowed(b, actcopy)
+        clear(t)
+        turn(A("aa", 0, 64), A("bc", 0, 64))
+        if t == 0:
+            ops.extend(last)
+        for j, k in enumerate(ranks):
+            ts(A("eqt", BLK * j, BLK * j + 64), A("aa", 0, 64), lc(k), ALU.is_equal, 2.0, ALU.mult)
+            ts(A("eqt", BLK * j + 64, BLK * j + 128), A("aa", 0, 64), lc(k), ALU.is_gt, 2.0, ALU.mult)
+        ends = A("sct", BLK - 1, nk * BLK, BLK)
+        count = [lambda: scan(A("sct", 0, nk * BLK), A("d0", 0, nk * BLK), A("eqt", 0, nk * BLK), 0.0, ALU.mult, ALU.add),
+                 lambda: tt(A("hh", 0, nk, 1, 0, 64), part(ends, 0, 64), part(ends, 64, 128), ALU.add),
+                 lambda: tt(A("cc", 0, nk, 1, 0, 32), A("hh", 0, nk, 1, 0, 32), A("hh", 0, nk, 1, 32, 64), ALU.add),
+                 lambda: [copy(A("cc", 0, nk, 1, 32 * q, 32 * q + 32), A("cc", 0, nk, 1, 0, 32)) for q in range(1, 4)],
+                 lambda: ts(A("bfl", 0, nr), ind(A("cc", 0, nk), off_spread), -1.0, ALU.max, 1.0, ALU.min),
+                 lambda: turn(A("sd", 16, 16 + nr), A("bfl", 0, nr))]
+        for f in count[:AT]:
+            f()
+        turn(A("pf", 16, 48), A("bn", 0, 32))
+        for f in count[AT:AT2]:
+            f()
+        wps = n("wps")
+        pick = lambda o, c0, cnt: scan(A(wps, o, o + cnt), A("rt", 0, cnt), A("pf", c0, c0 + cnt), 0.0, ALU.add, ALU.min)
+        to_left, to_right = A(wps, 15, 16), A(wps, 47, 48)
+        if left and back_of(r - 1) != back:
+            pick(48, 16 - back_of(r - 1), 16)
+            to_left = A(wps, 63, 64)
+        if right and back_of(r + 1) != back:
+            pick(48, 48 - back_of(r + 1), 16)
+            to_right = A(wps, 63, 64)
+        pick(0, 16 - back, NS)
         pp = []
         if left:
-            pp.append((r - 1, A(n("pw"), 0, 2), A(n("lp"), 2, 4) if r > 1 else A(n("lp"), 0, 2), False))
+            pp.append((r - 1, to_left, A(n("lp"), 8, 9), False))
         if right:
-            pp.append((r + 1, A(n("pw"), 0, 2), A(n("lp"), 0, 2), False))
+            pp.append((r + 1, to_right, A(n("lp"), 0, 1), False))
         w = send_sides(n("ap"), pp)
-        arrive(n("ap"), w * sides, [A(n("lp"), 0, 2 * sides)])
-        act(A("bn", 32, 64), ind(A(n("pw"), 0, 2), A("off", 2, 4)), ACT.Identity, bias=kcol, scale=-0.5)
-        borrowed(2, actcopy)
-        borrowed(3, actcopy)
-        landed = lambda k: spread(k, A(n("lc"), col(k), col(k) + 1))
-        order = others[::-1]
-        landed(order[0])
-        landed(order[1])
-        for j, k in enumerate(order):
-            if j + 2 < len(order):
-                landed(order[j + 2])
-            if j + 3 == len(order):
-                copy(A("bc", 256, 288), ind(A(n("lc"), 0, 11), A("off", 0, 2)))
-            turn(A("aa", 32 * k, 32 * k + 32), A("bc", 32 * k, 32 * k + 32))
-        if t == 0:
-            dma("sy", ap(A("vt", 0, 512)), T.v[:], [A("bc", 256, 288)], [A("vt", 0, 512)])
-        for c in range(nc):
-            v = A("bc", 256 + 16 * c, 257 + 16 * c)
-            act(A("junk", 256 * c, 256 * c + 256), A("aa", 0, 256), ACT.Sign, bias=v, scale=-1.0, acc=A("pp", c, c + 1))
-            ts(A("eqt", 256 * c, 256 * c + 256), A("aa", 0, 256), v, ALU.is_equal)
-        for c in range(nc):
-            scan(A("sct", 256 * c, 256 * c + 256), A("d0", 256 * c, 256 * c + 256), A("eqt", 256 * c, 256 * c + 256), 0.0, ALU.mult, ALU.add)
-        for c in range(nc):
-            ts(A("fl", c, c + 1), A("pp", c, c + 1), A("sct", 256 * c + 255, 256 * c + 256), ALU.is_ge, 2.0, ALU.mult)
-        turn_no = 0
-        for j, k in enumerate(ranks):
-            if k == extra:
-                continue
-            a = k - base
-            for q in range(4):
-                o, i, f = A("bfl", 32 * j, 32 * j + 32, 1, 32 * q, 32 * q + 32), A("neg", 0, 32, 1, 32 * a, 32 * a + 32), A("fl", 0, 1, 1, 32 * a, 32 * a + 32)
-                if turn_no % 2:
-                    ts(o, i, f, ALU.add)
-                else:
-                    act(o, i, ACT.Identity, bias=f)
-                turn_no += 1
-        if extra is not None:
-            j = ranks.index(extra)
-            ts(A("bfl", 32 * j, 32 * j + 32), A("neg", 0, 32), A("fl", 1, 2), ALU.add)
-        pfw = A(n("pf"), 16 + s0, 16 + s1)
-        lp = A(n("lp"), 0, 2 * sides)
-        if left:
-            act(A("bn", 0, 32), ind(lp, A("off", 2, 4)), ACT.Identity, bias=A("cf", 6, 7), scale=-0.5)
-        if right:
-            act(A("bn", 64, 96), ind(lp, A("off", 4, 6) if left else A("off", 2, 4)), ACT.Identity, bias=A("cf", 7, 8), scale=-0.5)
-        turn(A("sd", 0, nr), A("bfl", 0, nr))
-        sdw = A("sd", w0, w0 + ns)
-        act(A("dr", 0, ns), sdw, ACT.Identity, bias=0.5, scale=0.5)
-        if base:
-            comp("ve", lambda e: e.tensor_reduce(ap(A("tot", 0, 1)), ap(A("sd", 0, nr)), AxisListType.X, ALU.add), [A("sd", 0, nr)], [A("tot", 0, 1)])
-        tot = A("tot", 0, 1) if base else 0.0
-        scan(A("zs", 0, w0 + ns), A("sd", 0, w0 + ns), A("dp", 0, w0 + ns), 16.0 * nb0, ALU.add, ALU.add)
-        turn(A(n("pf"), 0, 96), A("bn", 0, 96))
-        zsw = A("zs", w0, w0 + ns)
-        if base:
-            ts(A("zt", 0, ns), zsw, tot, ALU.subtract)
-            zsw = A("zt", 0, ns)
+        arrive(n("ap"), w * sides, ([A(n("lp"), 0, 1)] if left else []) + ([A(n("lp"), 8, 9)] if right else []))
         if t == R - 1:
-            dma("sy", T.ol[:], T[n("pf")][0:128:16, 32:64], [A(n("pf"), 32, 64)], [])
-        zw = A("zz", 0, ns)
-        tt(A("zi", 0, ns), zsw, pfw, ALU.add)
-        scan(A("wp", 0, ns), A("rt", 0, ns), pfw, 0.0, ALU.add, ALU.min)
-        tt(zw, zsw, pfw, ALU.add)
-        ts(A("zb", 0, ns), A("zi", 0, ns), 15, ALU.bitwise_and)
-        ts(A(n("voff"), 0, 3), A("wp", 15, ns, 16), float(BW), ALU.add, *((float(FW - 1), ALU.min) if right else (0.0, ALU.max)))
-        tt(A("hd", 0, ns), A("hc", 0, ns), pfw, ALU.subtract)
-        for b in range(4):
-            actcopy(A(n("vtl"), b, 4 * ns, 4), ind(A(fh, PW * b, PW * b + FW), A(n("voff"), 0, 3)))
-        n4 = ns // 16
-        if base:
-            act(A("ini", 1, 2), tot, ACT.Identity, bias=inic)
+            act(A("junk2", 128, 160), A("pf", 16, 48), ACT.Identity, bias=-float(C * r), scale=0.5)
+            dma("sy", T.ol[:], T["junk2"][0:128:16, 128:160], [A("junk2", 128, 160)], [])
+        if t == 0:
+            dma("sy", ap(A("vt", 0, 512)), T.v[:], [A("lp0", 0, 9)], [A("vt", 0, 512)])
+        for f in count[AT2:]:
+            f()
+        own = A(wps, 15, 48, 16)
+        ts(A("wp", 0, 3), own, vcol, ALU.add)
+        scan(A("zs", z0, z1), A("sd", z0, z1), A("sd", z0, z1), zinit if low_half else 0.0, ALU.add, ALU.add)
+        scan(A("rr", 0, NS), A("mk", 0, NS), A("sd", w0, w0 + NS), 0.0, ALU.mult, ALU.add)
+        tt(A("tb", 0, 3), A("zs", w0 + 15, w0 + NS, 16), own, ALU.add)
+        if low_half:
+            ts(A("ta", 0, 3), A("rr", 15, NS, 16), scol, ALU.mult)
+        else:
+            ts(A("ta", 0, 3), A("rr", 15, NS, 16), scol, ALU.mult, A("zs", zl, zl + 1), ALU.subtract)
         if left:
-            act(A("ini", 0, 1), A("zs", w0 - 1, w0), ACT.Identity, bias=A("ini", 1, 2) if base else inic, scale=-1.0)
+            act(A("ini", 0, 1), A("zs", w0 - 1, w0) if low_half else A("zs", zl, zl + 1), ACT.Identity, bias=inic, scale=-0.5 if low_half else 0.5)
         ini = A("ini", 0, 1) if left else inic
-        scan(A("wz", 0, ns), A("rt", 0, ns), zw, 0.0, ALU.add, ALU.min)
-        ts(A("e2", 0, ns), A("zb", 0, ns), icol, ALU.is_lt)
-        ts(A("e1", 0, ns), A("zb", 0, ns), icol, ALU.is_equal)
-        tt(A("dh", 0, ns), A("dr", 0, ns), A("hd", 0, ns), ALU.mult)
-        copy(A("wi", 0, n4), A("wz", 15, ns, 16))
-        tt(A("x2", 0, ns), A("e2", 0, ns), sdw, ALU.mult)
-        tt(A("x1", 0, ns), A("e1", 0, ns), A("dh", 0, ns), ALU.mult)
-        ts(A("wa", 0, n4), A("wi", 0, n4), 4, ALU.arith_shift_right)
-        tt(A("x3", 0, ns), sdw, A("x2", 0, ns), ALU.subtract)
-        tt(A("vv", 0, ns), A("x1", 0, ns), A("x2", 0, ns), ALU.subtract)
-        ts(A("so", 0, n4), A("wa", 0, n4), 5.0, ALU.mult, m4a, ALU.add)
-        ts(A("so", n4, 2 * n4), A("wa", 0, n4), 5.0, ALU.mult, m4b, ALU.add)
-        tt(A("vv", ns, 2 * ns), A("x1", 0, ns), A("x3", 0, ns), ALU.add)
-        quant(A(n("qv"), 0, 128), A(n("sv"), 0, 128), A(n("vtl"), 0, 512))
+        voff = A(n("voff"), 0, 3)
+        to_v = lambda j: ts(A(n("voff"), j, j + 1), A("wp", j, j + 1), A(n("lp"), 4 * j, 4 * j + 1), ALU.add, 0.5, ALU.mult)
+        to_w = lambda j: ts(A("wi", j, j + 1), A("ta", j, j + 1), A("tb", j, j + 1), ALU.add, A(n("lp"), 4 * j, 4 * j + 1), ALU.add)
+        to_v(1)
+        to_v(0)
+        to_v(2)
+        for j in (1, 0, 2):
+            to_w(j)
+        gv = lambda move, b: move(A("vtl", b, 4 * NS, 4), ind(A(fh, PW * b, PW * b + FW), voff))
+        for b in range(VV, 4):
+            gv(actcopy, b)
+        for b in range(VV):
+            gv(copy, b)
+        ts(A("we", 0, 3), A("wi", 0, 3), 31, ALU.bitwise_and)
+        ts(A("wa", 0, 3), A("wi", 0, 3), 5, ALU.arith_shift_right)
+        tt(A("ha", 0, NS), ind(A("iof", 0, FW - 1), voff), A("iof", FW - 1, PW - 1), ALU.subtract)
+        copy(A("eo", 0, 3), A("we", 0, 3))
+        ts(A("so", 0, 3), A("wa", 0, 3), 5.0, ALU.mult, m4, ALU.add)
+        tt(A("hb", 0, NS), ind(A("iof", 0, FW - 1), voff), A("iof", FW, PW), ALU.subtract)
+        tt(A("vv1", 0, NS), ind(A("tab1", 0, 32), A("eo", 0, 3)), A("ha", 0, NS), ALU.max)
+        quant(A(n("qv"), 0, 128), A(n("sv"), 0, 128), A("vtl", 0, 512))
+        tt(A("vv2", 0, NS), ind(A("tab2", 0, 32), A("eo", 0, 3)), A("hb", 0, NS), ALU.max)
         for b in range(4):
-            layer(bank(1 + b, 128), b, A(n("qv"), 0, 128), A(n("sv"), 0, 128))
-            act(A(fh, PW * b + FW, PW * b + PW), bank(1 + b, ns), ACT.Relu, scale=0.03125)
-        copy(ind(A(n("win"), 0, 2 * WOFF), A("so", 0, 2 * n4)), A("vv", 0, 2 * ns))
-        scan(A("sc", 0, nscan), A(n("win"), 0, nscan), A(n("win"), WOFF, WOFF + nscan), ini, ALU.add, ALU.subtract)
-        copy(A(n("eoff"), 0, 28), A("sc", 5 * nb0 + 4, nscan, 5))
+            layer(bank(b, 128), b, A(n("qv"), 0, 128), A(n("sv"), 0, 128))
+            act(A(fh, PW * b + FW, PW * b + PW), bank(b, NS), ACT.Relu, scale=0.03125)
+        copy(ind(A(n("win"), 0, 320), A("so", 0, 3)), A("vv1", 0, NS))
+        copy(ind(A(n("wim"), 0, 320), A("so", 0, 3)), A("vv2", 0, NS))
+        scan(A("sc", 0, nscan), A(n("wim"), 0, nscan), A(n("win"), 5, nscan + 5), ini, ALU.add, ALU.subtract)
+        copy(A(n("eoff"), 0, 28), A("sc", 5 * nb - 1, nscan, 5))
         nq, nsc = "t%d" % (t + 1), "s%d" % (t + 1)
-        cols = lambda name, h: A(name, HALF * h, HALF * h + HALF)
-        plane = lambda name, h, b: A(name, 4 * HALF * h + b, 4 * HALF * (h + 1), 4)
-        src = lambda h, b: ind(A(fh, PW * b, PW * b + PW), A(n("eoff"), 14 * h, 14 * h + 14))
         etl, xn = n("etl"), n("xn")
-        qe = lambda h: quant(cols(n("qe"), h), cols(n("se"), h), A(etl, 4 * HALF * h, 4 * HALF * (h + 1)))
-        rl = lambda h, b: A("rl", HALF * (4 * h + b), HALF * (4 * h + b + 1))
+        cols = lambda name, h: A(name, *PIECES[h])
+        wide = lambda h: PIECES[h][1] - PIECES[h][0]
+        tile = lambda name, h: A(name, 4 * PIECES[h][0], 4 * PIECES[h][1])
+        plane = lambda name, h, b: A(name, 4 * PIECES[h][0] + b, 4 * PIECES[h][1], 4)
+        gather = lambda move, h, b: move(plane(etl, h, b), ind(A(fh, PW * b, PW * b + PW), A(n("eoff"), PIECES[h][0] // 16, PIECES[h][1] // 16)))
+        qe = lambda h: quant(cols(n("qe"), h), cols(n("se"), h), tile(etl, h))
+        qx = lambda h: quant(cols(nq, h), cols(nsc, h), tile(xn, h))
+        rl = lambda h, b: A("rl", C * b + PIECES[h][0], C * b + PIECES[h][1])
+        relu = lambda h, b: act(rl(h, b), bank(4 + b, wide(h)), ACT.Relu, scale=0.015625)
+        add = lambda h, b: tt(plane(xn, h, b), bank(b, wide(h)), rl(h, b), ALU.add)
 
         def products(h, b):
-            layer(bank(4 + b, HALF), b, cols(n("qe"), h), cols(n("se"), h))
-            unpack(bank(b, HALF), b, cols(n("qe"), h), cols(n("se"), h))
-        for b in range(2):
-            copy(plane(etl, 0, b), src(0, b))
-            actcopy(plane(etl, 0, 2 + b), src(0, 2 + b))
-        qe(0)
-        for b in range(4):
-            products(0, b)
-        copy(plane(etl, 1, 0), src(1, 0))
-        for b in range(1, 4):
-            actcopy(plane(etl, 1, b), src(1, b))
-        ts(rl(0, 0), bank(4, HALF), 0.0, ALU.max, 0.015625, ALU.mult)
-        for h in range(2):
-            for b in range(4):
-                if h or b:
-                    act(rl(h, b), bank(4 + b, HALF), ACT.Relu, scale=0.015625)
-                tt(plane(xn, h, b), bank(b, HALF), rl(h, b), ALU.add)
-                if h == 0:
-                    if b == 0:
-                        qe(1)
-                    products(1, b)
-            quant(cols(nq, h), cols(nsc, h), A(xn, 4 * HALF * h, 4 * HALF * (h + 1)))
+            layer(bank(4 + b, wide(h)), b, cols(n("qe"), h), cols(n("se"), h))
+            unpack(bank(b, wide(h)), b, cols(n("qe"), h), cols(n("se"), h))
+        vrelu = lambda h, b: ts(rl(h, b), bank(4 + b, wide(h)), 0.0, ALU.max, 0.015625, ALU.mult)
+        calls = {"g": lambda h, b: gather(copy, h, b), "G": lambda h, b: gather(actcopy, h, b), "e": lambda h, b: qe(h), "x": lambda h, b: qx(h),
+                 "p": products, "R": relu, "r": vrelu, "a": add,
+                 "w": lambda h, b: layer(bank(4 + b, wide(h)), b, cols(n("qe"), h), cols(n("se"), h)),
+                 "u": lambda h, b: unpack(bank(b, wide(h)), b, cols(n("qe"), h), cols(n("se"), h))}
+        for word in TAIL.split():
+            calls[word[0]](int(word[1]), int(word[2:] or 0))
 
-    for h in range(2):
-        c0, c1 = HALF * h, HALF * h + HALF
+    for h, (c0, c1) in enumerate([(0, PIECES[-1][0]), PIECES[-1]]):
         dma("sy", T.oc[:, 4 * c0:4 * c1], b8(A("t2", c0, c1)), [A("t2", c0, c1)], [])
-        mm(bank(h, HALF), A("vq", 0, 128), A("vs", 0, 128), A("t2", c0, c1), A("s2", c0, c1))
-        actcopy(A("ys", c0, c1), bank(h, HALF))
+        mm(bank(4 + h, c1 - c0), A("vq", 0, 128), A("vs", 0, 128), A("t2", c0, c1), A("s2", c0, c1))
+        actcopy(A("ys", c0, c1), bank(4 + h, c1 - c0))
         dma("se", T.y[:, c0:c1], ap(A("ys", c0, c1)), [A("ys", c0, c1)], [])
     for k in range(4):
         dma("sy", T.osc[4 * k:4 * k + 4, 0:C], T.s2[32 * k:32 * k + 4, 0:C], [A("s2", 0, C)], [])

@@ -11,9 +11,12 @@ ROW = 48
 EB = 7 * ROW
 AT, AT2, VV = 0, 1, 1
 BLK = 129
-TAIL = ("g00 G02 g01 G03 g10 e0 G12 G13 p00 p01 p02 p03 g11 G22 e1 g20 R00 a00 w10 R01 a01 w11 u10 G23 g21 R02 a02 w12 u11 R03 a03 w13 u12 u13 e2 "
+HALVES, ALL = True, True
+TAIL = ("g00 G02 o0 g01 G03 g10 e0 G12 G13 p00 p01 p02 p03 g11 G22 e1 g20 R00 a00 w10 R01 a01 w11 u10 G23 g21 R02 a02 w12 u11 R03 a03 w13 u12 u13 e2 "
         "R10 a10 w20 R11 a11 w21 u20 x0 R12 a12 w22 u21 R13 a13 w23 u22 u23 R20 a20 x1 R21 a21 R22 a22 R23 a23 x2")
 CUTS = [(0, 320), (320, 448)]
+WP, SPLIT = 1, True
+BOR, BOR2, QV = 3, 4, 1
 FIRST = False
 EARLY = 6
 ORDER = True
@@ -30,11 +33,11 @@ for _n, _w, _d in [("xt", 4 * C, BF), ("ut", 512, BF), ("vt", 512, BF), ("uq", 1
                    ("eqt", 5 * BLK + 1, BF), ("sct", 5 * BLK + 1, BF),
                    ("off", 24, U16), ("uoff", 8, U16), ("so", 4, U16), ("eo", 4, U16), ("pi", 8, I32),
                    ("pj", 8, I32), ("pl", 8, I32), ("wi", 4, I32), ("wa", 4, I32), ("we", 4, I32), ("t2", C, Q4), ("s2", C, U8),
-                   ("vtl", 512, BF)]:
+                   ("vtl", 512, BF), ("tab", 2048, BF)]:
     SCRATCH[_n] = ("sbuf", [128, _w], _d)
-for _w, _ns in [(4, "ini wp ta tb tc"), (8, "pk ms0 hh cc"), (16, "pc nst cm cf lt16 hf"), (32, "bn tab1 tab2"),
-                (48, "mk ha hb vv1 vv2 rr"), (64, "rt bc aa"), (96, "pf df"), (112, "io16 thc tx ty tz th u1 u2 u3 th2"),
-                (160, "bfl junk2"), (208, "sd zs"), (320, "sc"), (C, "ys"), (PW, "iof"), (4 * C, "rl"),
+for _w, _ns in [(4, "ini wp ta tb tc"), (8, "pk ms0 cc"), (16, "pc nst cm cf lt16 hf"), (24, "hh cc4 m4"), (32, "bn"),
+                (48, "mk ha hb vv1 vv2 rr"), (64, "rt bc aa"), (96, "pf"), (112, "io16 thc tx ty tz u1 u2 u3"), (224, "th th2"),
+                (160, "bfl"), (288, "junk2"), (208, "sd zs"), (320, "sc"), (C, "ys"), (PW, "iof"), (4 * C, "rl"),
                 (EB + 32 * ROW, "om")]:
     for _n in _ns.split():
         SCRATCH[_n] = ("sbuf", [128, _w], F32)
@@ -254,6 +257,7 @@ def rank_program(g, core, T, topo):
     reach = lambda k: max(0, min(N * S // 2, k + 1, N * S - 1 - k))
     nb = -(-(L * back + reach(k0)) // 16) + 1
     nscan = 5 * (nb + 27)
+    ntab = 2 * (16 * nb + L * (NS - back) + reach(k0 + NS - 1))
     z0 = w0 if (r == 0 or not low_half) else 16
     zl = 16 + nr + (0 if right else 16 - back)
     z1 = w0 + NS if low_half else zl + 1
@@ -292,16 +296,16 @@ def rank_program(g, core, T, topo):
     copy(A("pk", 0, 5), A("pl", 0, 5))
     ts(A("ms0", 4, 8), A("pj", 4, 8), -1.0, ALU.mult, 7.0, ALU.add)
     ts(A("uoff", 0, 4), A("pj", 0, 4), 16.0, ALU.mult)
-    ts(mx, icol, float(back), ALU.is_ge, PAD, ALU.mult)
     tt(A("ms0", 0, 4), A("ms0", 4, 8), A("pj", 4, 8), ALU.max)
+    ts(mx, icol, float(back), ALU.is_ge, PAD, ALU.mult)
     ts(A("rt", 0, 64), io(0, 64), icol, ALU.is_equal, TALL, ALU.mult)
     ts(A("lt16", 0, 16), io(0, 16), icol, ALU.is_lt)
     ts(A("uoff", 4, 8), A("ms0", 0, 4), 16.0, ALU.mult)
     memset(A("d0", 0, nk * BLK), 1.0)
-    memset(A("om", EB, EB + 8 * ROW, 3), BIG)
-    memset(A("om", EB + 1, EB + 8 * ROW, 3), 0.0)
-    for c0 in (2, ROW - 3, ROW - 1):
-        memset(A("om", c0, EB + 8 * ROW, ROW), BIG)
+    fill(A("om", EB, EB + 8 * ROW, 3), BIG)
+    fill(A("om", EB + 1, EB + 8 * ROW, 3), 0.0)
+    for c0 in (2, ROW - 1, ROW - 3):
+        fill(A("om", c0, EB + 8 * ROW, ROW), BIG)
     actcopy(A("eb", 2, 514, 4), A("idn", 0, 128))
     actcopy(A("eb", 523, 1035, 4), A("idn", 0, 128))
     quant(A("uq", 0, 128), A("us", 0, 128), A("ut", 0, 512))
@@ -314,18 +318,18 @@ def rank_program(g, core, T, topo):
         c0 = 520 * (b % 2) + 2 - 2 * (b // 2)
         quant(A("eq", 128 * b, 128 * b + 128), A("es", 128 * b, 128 * b + 128), A("eb", c0, c0 + 512))
 
-    act(A("thc", 16, 112), io(16, 112), ACT.Identity, bias=-8.0)
+    act(A("thc", 16, 112), io(16, 112), ACT.Identity, bias=-1.0)
     act(A("thc", 0, 16), io(0, 16), ACT.Identity, bias=-1.5)
+    fill(A("th", 1, 224, 2), -TALL)
+    fill(A("th2", 1, 224, 2), -TALL)
     first, ops = ops, []
-    act(kc2, kcol, ACT.Identity, bias=13.0 + 2 * C * r, scale=2.0 * L)
+    act(kc2, kcol, ACT.Identity, bias=2.0 * C * r - 1.0, scale=2.0 * L)
     act(vcol, mx, ACT.Identity, bias=2.0 * (BW - C * r), scale=-1.0)
     act(zinit, mx, ACT.Identity, bias=32.0 * nb - 2 * C * r + 0.5 + (0 if left else 2 * back), scale=-1.0)
     act(scol, A("rt", 15, 16), ACT.Identity, bias=-2.0, scale=2.5 / TALL)
     act(A("ha", 0, NS), A("rt", 16, 64), ACT.Identity, bias=1.0, scale=-1.0 / TALL)
     act(A("hb", 0, NS), A("rt", 15, 63), ACT.Identity, scale=1.25 / TALL)
     act(inic, vcol, ACT.Identity, bias=icol, scale=0.5) if left else act(inic, icol, ACT.Identity, bias=float(BW - 16 * nb - back))
-    act(A("tab1", 0, 32, 2), A("lt16", 0, 16), ACT.Identity, scale=-1.0)
-    act(A("tab2", 0, 32, 2), A("lt16", 0, 16), ACT.Identity, bias=1.0, scale=-1.0)
     for j, k in enumerate(ranks):
         a = k // 2
         c0 = BLK * j + 32 * (k % 2)
@@ -352,17 +356,28 @@ def rank_program(g, core, T, topo):
         act(A("wim%d" % t, 0, nscan), A("iof", 0, nscan), ACT.Identity, scale=0.0)
         fill(A("win%d" % t, 4, nscan + 5, 5), -16.0)
     later, ops = ops, []
-    memset(A("vtl", 4 * NS, 512), 0.0)
+    twice = lambda w: copy(A("tab", w, 2 * w), A("tab", 0, w))
+    ts(A("tab", 0, 32, 2), A("lt16", 0, 16), -1.0, ALU.mult)
+    tt(A("tab", 1, 32, 2), A("lt16", 0, 16), A("rt", 0, 16), ALU.subtract)
+    twice(32)
     ts(A("wi", 0, 4), A("hf", 0, 4), quad2, ALU.add, float(N - r), ALU.add)
-    ts(off_pair, io(0, 2), quad2, ALU.add)
+    twice(64)
     ts(A("wa", 0, 4), A("wi", 0, 4), N - 1, ALU.bitwise_and)
-    copy(off_spread, A("hf", 0, 2 * nk))
+    twice(128)
+    ts(off_pair, io(0, 2), quad2, ALU.add)
+    twice(256)
     ts(off_rank, A("wa", 0, 4), 3.0, ALU.add)
+    if ALL:
+        ts(off_spread, A("hf", 0, 2 * nk), 4.0, ALU.mult, 3.0, ALU.add)
+        memset(A("m4", 0, 20), 1.0)
+    else:
+        copy(off_spread, A("hf", 0, 2 * nk))
     ts(A("d0", 64, nk * BLK, BLK), A("hf", ranks[0], ranks[0] + nk), quad, ALU.is_le)
-    tt(A("tab1", 1, 32, 2), A("lt16", 0, 16), A("rt", 0, 16), ALU.subtract)
     for t in range(R):
         memset(A("lc%d" % t, 0, 3), 0.0)
-    ts(A("tab2", 1, 32, 2), A("tab1", 1, 32, 2), -1.0, ALU.add)
+    memset(A("vtl", 4 * NS, 512), 0.0)
+    if ALL:
+        memset(A("m4", 0, 20, 4), 0.0)
     if sides == 1:
         ts(cf(13), icol, float(back), ALU.is_ge if left else ALU.is_lt)
     spare, ops = ops, []
@@ -425,6 +440,9 @@ def rank_program(g, core, T, topo):
             gap(2)
         pair(3)
         gap(2)
+        if t == 0:
+            for c0 in range(512, ntab, 512):
+                actcopy(A("tab", c0, min(ntab, c0 + 512)), A("tab", 0, min(ntab - c0, 512)))
         lo3 = om(o_(3) + 10, 13)
         cost = A(n("lc"), 3, 4)
         step(4)
@@ -454,13 +472,12 @@ def rank_program(g, core, T, topo):
         tx = lambda a, b: tt(A("tx", a, b), om(o6 + 3 * a + 2, b - a), om(o6 + 3 * a + 10, b - a), ALU.is_le)
         ty = lambda a, b: tt(A("ty", a, b), om(o6 + 3 * a + 4, b - a), om(o6 + 3 * a + 5, b - a), ALU.is_le)
         tz = lambda a, b: tt(A("tz", a, b), A("tx", a, b), A("thc", a, b), ALU.add)
-        th = lambda a, b: tt(A("th", a, b), A("tz", a, b), A("ty", a, b), ALU.add)
-        two = lambda o, a, b, op, c0, c1: tt(A(o, c0, c1), A(a[0], c0 + a[1], c1 + a[1]), A(b[0], c0 + b[1], c1 + b[1]), op)
-        df = lambda c0, c1: two("df", ("th", 1), ("th", 0), ALU.subtract, c0, c1)
-        u1 = lambda c0, c1: two("u1", ("ty", 0), ("df", -17), ALU.mult, c0, c1)
-        u2 = lambda c0, c1: two("u2", ("tx", 0), ("df", -16), ALU.mult, c0, c1)
-        u3 = lambda c0, c1: two("u3", ("u1", 0), ("th", -17), ALU.add, c0, c1)
-        th2 = lambda c0, c1: two("th2", ("u3", 0), ("u2", 0), ALU.add, c0, c1)
+        even = lambda name, a, b: A(name, 2 * a, 2 * b - 1, 2)
+        th = lambda a, b: tt(even("th", a, b), A("tz", a, b), A("ty", a, b), ALU.add)
+        u1 = lambda a, b: tt(A("u1", a, b), A("ty", a, b), even("th", a - 16, b - 16), ALU.mult)
+        u2 = lambda a, b: tt(A("u2", a, b), A("tx", a, b), even("th", a - 15, b - 15), ALU.mult)
+        u3 = lambda a, b: tt(A("u3", a, b), A("u1", a, b), A("u2", a, b), ALU.max)
+        th2 = lambda a, b: tt(even("th2", a, b), A("u3", a, b), even("th", a - 17, b - 17), ALU.max)
         spread = lambda: copy(A("bc", 0, 64), ind(A(n("lc"), 0, 3 + N), off_rank))
         pair(4)
         tx(48, 111)
@@ -472,24 +489,22 @@ def rank_program(g, core, T, topo):
         step(6)
         tx(16, 47)
         ty(16, 47)
-        df(48, 94)
         pair(6)
         tz(16, 47)
         u1(65, 110)
+        u2(65, 110)
         step(7)
         tx(1, 14)
         th(16, 47)
         ty(1, 14)
         scan(A("pc", 0, L), om(5, L), om(5, L), BIG, ALU.min, ALU.min)
         tz(1, 14)
-        df(16, 30)
-        u2(65, 110)
-        u3(65, 110)
-        th(1, 14)
         u1(33, 46)
         u2(33, 46)
-        th2(65, 110)
+        u3(65, 110)
+        th(1, 14)
         u3(33, 46)
+        th2(65, 110)
         gap(len(spare))
         if FIRST:
             spread()
@@ -500,14 +515,14 @@ def rank_program(g, core, T, topo):
         act(A("junk2", 0, L, 1, 0, 64), A("pc", 0, L, 1, 0, 64), ACT.Sign, bias=part(cost, 0, 64), scale=-1.0, acc=nst(8))
 
         def back_to(k, frm, name):
-            o = 16 * (6 - k)
-            act(A("junk2", 16 * k + 16, 16 * k + 29, 1, 0, 64), A(name, o + 1, o + L, 1, 0, 64), ACT.Sign, bias=nst(frm),
+            o = 32 * (6 - k) + 1
+            act(A("junk2", 32 * k + 32, 32 * k + 59, 1, 0, 64), A(name, o, o + 27, 1, 0, 64), ACT.Sign, bias=nst(frm),
                 scale=1.0 if frm == 8 else 2.0, acc=nst(k))
         lc = lambda k: A(n("lc"), col(k), col(k) + 1)
         if WLATE and t == 0:
             load_w([nst(8)])
         back_to(6, 8, "th")
-        act(nst(7), nst(8), ACT.Identity, bias=13.0, scale=2.0)
+        act(nst(7), nst(8), ACT.Identity, bias=-1.0, scale=2.0)
         back_to(4, 6, "th2")
         back_to(5, 6, "th")
         back_to(2, 4, "th2")
@@ -516,9 +531,8 @@ def rank_program(g, core, T, topo):
         back_to(0, 2, "th2")
         back_to(1, 2, "th")
         act(A("bn", 0, 32), ind(A("nst", 0, 8), off_pair), ACT.Identity, bias=kc2, scale=-1.0)
-        for b in range(4):
+        for b in range(BOR):
             borrowed(b, actcopy)
-        clear(t)
         turn(A("aa", 0, 64), A("bc", 0, 64))
         if t == 0:
             ops.extend(last)
@@ -526,12 +540,25 @@ def rank_program(g, core, T, topo):
             ts(A("eqt", BLK * j, BLK * j + 64), A("aa", 0, 64), lc(k), ALU.is_equal, 2.0, ALU.mult)
             ts(A("eqt", BLK * j + 64, BLK * j + 128), A("aa", 0, 64), lc(k), ALU.is_gt, 2.0, ALU.mult)
         ends = A("sct", BLK - 1, nk * BLK, BLK)
+
+        def flags():
+            j = (nk + 1) // 2 if SPLIT else nk
+            cc = A("cc4", 0, 4 * nk) if ALL else A("cc", 0, nk)
+            ts(A("bfl", 0, S * j), ind(cc, A("off", 6, 6 + 2 * j)), -1.0, ALU.max, 1.0, ALU.min)
+            if j < nk:
+                act(A("bfl", S * j, nr), ind(cc, A("off", 6 + 2 * j, 6 + 2 * nk)), ACT.Sign)
         count = [lambda: scan(A("sct", 0, nk * BLK), A("d0", 0, nk * BLK), A("eqt", 0, nk * BLK), 0.0, ALU.mult, ALU.add),
                  lambda: tt(A("hh", 0, nk, 1, 0, 64), part(ends, 0, 64), part(ends, 64, 128), ALU.add),
                  lambda: tt(A("cc", 0, nk, 1, 0, 32), A("hh", 0, nk, 1, 0, 32), A("hh", 0, nk, 1, 32, 64), ALU.add),
-                 lambda: [copy(A("cc", 0, nk, 1, 32 * q, 32 * q + 32), A("cc", 0, nk, 1, 0, 32)) for q in range(1, 4)],
-                 lambda: ts(A("bfl", 0, nr), ind(A("cc", 0, nk), off_spread), -1.0, ALU.max, 1.0, ALU.min),
+                 lambda: [(copy if q < 3 or not SPLIT else actcopy)(A("cc", 0, nk, 1, 32 * q, 32 * q + 32), A("cc", 0, nk, 1, 0, 32)) for q in range(1, 4)],
+                 flags,
                  lambda: turn(A("sd", 16, 16 + nr), A("bfl", 0, nr))]
+        if ALL:
+            def share():
+                moves = [(0, 128, 0, 0), (0, 64, 64, 1), (64, 128, 0, 1)] + [(32 * q, 32 * q + 32, 32 * (q ^ x), 1 + (x + 1) // 2) for x in (1, 3) for q in range(4)]
+                for i, (p0, p1, q0, slot) in enumerate(moves):
+                    (actcopy if i % 2 else copy)(A("hh", slot, 4 * nk, 4, q0, q0 + p1 - p0), part(ends, p0, p1))
+            count[1:4] = [share, lambda: scan(A("cc4", 0, 4 * nk), A("m4", 0, 4 * nk), A("hh", 0, 4 * nk), 0.0, ALU.mult, ALU.add)]
         for f in count[:AT]:
             f()
         turn(A("pf", 16, 48), A("bn", 0, 32))
@@ -554,17 +581,29 @@ def rank_program(g, core, T, topo):
             pp.append((r + 1, to_right, A(n("lp"), 0, 1), False))
         w = send_sides(n("ap"), pp)
         arrive(n("ap"), w * sides, ([A(n("lp"), 0, 1)] if left else []) + ([A(n("lp"), 8, 9)] if right else []))
-        if t == R - 1:
-            act(A("junk2", 128, 160), A("pf", 16, 48), ACT.Identity, bias=-float(C * r), scale=0.5)
-            dma("sy", T.ol[:], T["junk2"][0:128:16, 128:160], [A("junk2", 128, 160)], [])
         if t == 0:
             dma("sy", ap(A("vt", 0, 512)), T.v[:], [A("lp0", 0, 9)], [A("vt", 0, 512)])
         for f in count[AT2:]:
             f()
-        own = A(wps, 15, 48, 16)
+            if f == count[1]:
+                for b in range(BOR, BOR2):
+                    borrowed(b, actcopy)
+        for b in range(BOR2, 4):
+            borrowed(b, actcopy)
+        clear(t)
+        own, voff, sdw = A(wps, 15, 48, 16), A(n("voff"), 0, 3), A("sd", w0, w0 + NS)
+        land = lambda j: A(n("lp"), 4 * j, 4 * j + 1)
+        to_v = lambda j: ts(A(n("voff"), j, j + 1), A("wp", j, j + 1), land(j), ALU.add, 0.5, ALU.mult)
+        to_e = lambda j: ts(A("eo", j, j + 1), A("ta", j, j + 1), A("tb", j, j + 1), ALU.add, land(j), ALU.add)
+        gv = lambda move, b: move(A("vtl", b, 4 * NS, 4), ind(A(fh, PW * b, PW * b + FW), voff))
+        ha = lambda: tt(A("ha", 0, NS), ind(A("iof", 0, FW - 1), voff), A("iof", FW - 1, PW - 1), ALU.subtract)
         ts(A("wp", 0, 3), own, vcol, ALU.add)
         scan(A("zs", z0, z1), A("sd", z0, z1), A("sd", z0, z1), zinit if low_half else 0.0, ALU.add, ALU.add)
-        scan(A("rr", 0, NS), A("mk", 0, NS), A("sd", w0, w0 + NS), 0.0, ALU.mult, ALU.add)
+        scan(A("rr", 0, NS), A("mk", 0, NS), sdw, 0.0, ALU.mult, ALU.add)
+        to_v(1)
+        if WP == 0:
+            to_v(0)
+            to_v(2)
         tt(A("tb", 0, 3), A("zs", w0 + 15, w0 + NS, 16), own, ALU.add)
         if low_half:
             ts(A("ta", 0, 3), A("rr", 15, NS, 16), scol, ALU.mult)
@@ -573,35 +612,42 @@ def rank_program(g, core, T, topo):
         if left:
             act(A("ini", 0, 1), A("zs", w0 - 1, w0) if low_half else A("zs", zl, zl + 1), ACT.Identity, bias=inic, scale=-0.5 if low_half else 0.5)
         ini = A("ini", 0, 1) if left else inic
-        voff = A(n("voff"), 0, 3)
-        to_v = lambda j: ts(A(n("voff"), j, j + 1), A("wp", j, j + 1), A(n("lp"), 4 * j, 4 * j + 1), ALU.add, 0.5, ALU.mult)
-        to_w = lambda j: ts(A("wi", j, j + 1), A("ta", j, j + 1), A("tb", j, j + 1), ALU.add, A(n("lp"), 4 * j, 4 * j + 1), ALU.add)
-        to_v(1)
-        to_v(0)
-        to_v(2)
-        for j in (1, 0, 2):
-            to_w(j)
-        gv = lambda move, b: move(A("vtl", b, 4 * NS, 4), ind(A(fh, PW * b, PW * b + FW), voff))
+        if WP == 1:
+            to_v(0)
+            to_v(2)
+        if WP == 0:
+            ha()
         for b in range(VV, 4):
             gv(actcopy, b)
+        for j in (1, 0, 2):
+            to_e(j)
+        if WP == 1:
+            ha()
         for b in range(VV):
             gv(copy, b)
-        ts(A("we", 0, 3), A("wi", 0, 3), 31, ALU.bitwise_and)
-        ts(A("wa", 0, 3), A("wi", 0, 3), 5, ALU.arith_shift_right)
-        tt(A("ha", 0, NS), ind(A("iof", 0, FW - 1), voff), A("iof", FW - 1, PW - 1), ALU.subtract)
-        copy(A("eo", 0, 3), A("we", 0, 3))
+        ts(A("wa", 0, 3), A("eo", 0, 3), 1.0 / 32, ALU.mult, -31.0 / 64, ALU.add)
+        tt(A("vv1", 0, NS), ind(A("tab", 0, ntab), A("eo", 0, 3)), A("ha", 0, NS), ALU.max)
+        if QV == 0:
+            quant(A(n("qv"), 0, 128), A(n("sv"), 0, 128), A("vtl", 0, 512))
         ts(A("so", 0, 3), A("wa", 0, 3), 5.0, ALU.mult, m4, ALU.add)
-        tt(A("hb", 0, NS), ind(A("iof", 0, FW - 1), voff), A("iof", FW, PW), ALU.subtract)
-        tt(A("vv1", 0, NS), ind(A("tab1", 0, 32), A("eo", 0, 3)), A("ha", 0, NS), ALU.max)
-        quant(A(n("qv"), 0, 128), A(n("sv"), 0, 128), A("vtl", 0, 512))
-        tt(A("vv2", 0, NS), ind(A("tab2", 0, 32), A("eo", 0, 3)), A("hb", 0, NS), ALU.max)
+        if QV == 1:
+            quant(A(n("qv"), 0, 128), A(n("sv"), 0, 128), A("vtl", 0, 512))
+        if t == R - 1:
+            act(A("junk2", 256, 288), A("pf", 16, 48), ACT.Identity, bias=-float(C * r), scale=0.5)
+            dma("sy", T.ol[:], T["junk2"][0:128:16, 256:288], [A("junk2", 256, 288)], [])
+        tt(A("vv2", 0, NS), A("vv1", 0, NS), sdw, ALU.subtract)
         for b in range(4):
             layer(bank(b, 128), b, A(n("qv"), 0, 128), A(n("sv"), 0, 128))
             act(A(fh, PW * b + FW, PW * b + PW), bank(b, NS), ACT.Relu, scale=0.03125)
         copy(ind(A(n("win"), 0, 320), A("so", 0, 3)), A("vv1", 0, NS))
         copy(ind(A(n("wim"), 0, 320), A("so", 0, 3)), A("vv2", 0, NS))
-        scan(A("sc", 0, nscan), A(n("wim"), 0, nscan), A(n("win"), 5, nscan + 5), ini, ALU.add, ALU.subtract)
-        copy(A(n("eoff"), 0, 28), A("sc", 5 * nb - 1, nscan, 5))
+        m0 = PIECES[0][1] // 16 if HALVES else 28
+        n0 = 5 * (nb + m0 - 1)
+        scan(A("sc", 0, n0), A(n("wim"), 0, n0), A(n("win"), 5, n0 + 5), ini, ALU.add, ALU.subtract)
+        copy(A(n("eoff"), 0, m0), A("sc", 5 * nb - 1, n0, 5))
+        if HALVES:
+            scan(A("sc", n0, nscan), A(n("wim"), n0, nscan), A(n("win"), n0 + 5, nscan + 5), A("sc", n0 - 1, n0), ALU.add, ALU.subtract)
+        rest = lambda h, b: copy(A(n("eoff"), m0, 28), A("sc", n0 + 4, nscan, 5)) if HALVES else None
         nq, nsc = "t%d" % (t + 1), "s%d" % (t + 1)
         etl, xn = n("etl"), n("xn")
         cols = lambda name, h: A(name, *PIECES[h])
@@ -620,7 +666,7 @@ def rank_program(g, core, T, topo):
             unpack(bank(b, wide(h)), b, cols(n("qe"), h), cols(n("se"), h))
         vrelu = lambda h, b: ts(rl(h, b), bank(4 + b, wide(h)), 0.0, ALU.max, 0.015625, ALU.mult)
         calls = {"g": lambda h, b: gather(copy, h, b), "G": lambda h, b: gather(actcopy, h, b), "e": lambda h, b: qe(h), "x": lambda h, b: qx(h),
-                 "p": products, "R": relu, "r": vrelu, "a": add,
+                 "p": products, "R": relu, "r": vrelu, "a": add, "o": rest,
                  "w": lambda h, b: layer(bank(4 + b, wide(h)), b, cols(n("qe"), h), cols(n("se"), h)),
                  "u": lambda h, b: unpack(bank(b, wide(h)), b, cols(n("qe"), h), cols(n("se"), h))}
         for word in TAIL.split():

from concourse.bass import DstId, RemoteDMATransfer
from concourse.mybir import dt, AluOpType, AxisListType, ActivationFunctionType

N, C, S, L, R = 8, 448, 32, 14, 2
PIECES = [(0, 128), (128, 320), (320, 448)]
BW = 128
FW = C + 2 * BW
NS = 48
PW = FW + NS
ROW = 48
EB = 7 * ROW
AT, AT2, VV = 0, 1, 1
BLK = 129
HALVES, ALL = True, True
TAIL = ("g00 G02 o0 g01 G03 g10 e0 G12 G13 p00 p01 p02 p03 g11 G22 e1 g20 R00 a00 w10 R01 a01 w11 u10 G23 g21 R02 a02 w12 u11 R03 a03 w13 u12 u13 e2 "
        "R10 a10 w20 R11 a11 w21 u20 x0 R12 a12 w22 u21 R13 a13 w23 u22 u23 R20 a20 x1 R21 a21 R22 a22 R23 a23 x2")
CUTS = [(0, 320), (320, 448)]
WP, SPLIT = 1, True
BOR, BOR2, QV = 3, 4, 1
FIRST = False
EARLY = 6
ORDER = True
WLATE = True
PAD = 16384.0
TALL = 2.0 ** 20
BIG = 1.0e29
Q4, U8, BF, F32, I32, U16 = "float8_e4m3fn_x4", "uint8", "bfloat16", "float32", "int32", "uint16"

SCRATCH = {"ps": ("psum", [128, 4096], F32)}
for _n, _w, _d in [("xt", 4 * C, BF), ("ut", 512, BF), ("vt", 512, BF), ("uq", 128, Q4), ("us", 128, U8), ("uq2", 128, Q4),
                   ("us2", 128, U8), ("vq", 128, Q4), ("vs", 128, U8), ("wq", 512, Q4), ("wsc", 512, U8), ("eb", 1040, BF),
                   ("eq", 512, Q4), ("es", 512, U8), ("one", 512, BF), ("idn", 128, BF), ("d0", 5 * BLK + 1, BF),
                   ("eqt", 5 * BLK + 1, BF), ("sct", 5 * BLK + 1, BF),
                   ("off", 24, U16), ("uoff", 8, U16), ("so", 4, U16), ("eo", 4, U16), ("pi", 8, I32),
                   ("pj", 8, I32), ("pl", 8, I32), ("wi", 4, I32), ("wa", 4, I32), ("we", 4, I32), ("t2", C, Q4), ("s2", C, U8),
                   ("vtl", 512, BF), ("tab", 2048, BF)]:
    SCRATCH[_n] = ("sbuf", [128, _w], _d)
for _w, _ns in [(4, "ini wp ta tb tc"), (8, "pk ms0 cc"), (16, "pc nst cm cf lt16 hf"), (24, "hh cc4 m4"), (32, "bn"),
                (48, "mk ha hb vv1 vv2 rr"), (64, "rt bc aa"), (96, "pf"), (112, "io16 thc tx ty tz u1 u2 u3"), (224, "th th2"),
                (160, "bfl"), (288, "junk2"), (208, "sd zs"), (320, "sc"), (C, "ys"), (PW, "iof"), (4 * C, "rl"),
                (EB + 32 * ROW, "om")]:
    for _n in _ns.split():
        SCRATCH[_n] = ("sbuf", [128, _w], F32)
for _t in range(R):
    for _n, _w, _d in [("t", C, Q4), ("s", C, U8), ("lt", 2 * BW, Q4), ("ls", 2 * BW, U8), ("fh", 4 * PW, BF),
                       ("lc", 16, F32), ("lp", 12, F32), ("wps", 64, F32), ("voff", 4, U16),
                       ("qv", 128, Q4), ("sv", 128, U8), ("win", 320, F32), ("wim", 320, F32), ("eoff", 28, U16), ("etl", 4 * C, BF),
                       ("qe", C, Q4), ("se", C, U8), ("xn", 4 * C, BF)]:
        SCRATCH[_n + str(_t)] = ("sbuf", [128, _w], _d)

SEMAPHORES = (["pe", "ve", "se", "ge"] + ["d%d" % i for i in range(40)] + [a + str(t) for t in range(R) for a in ("at", "ap", "ac")])


def A(name, c0, c1, step=1, p0=0, p1=128):
    return (name, p0, p1, c0, c1, step)


def bank(b, n):
    return A("ps", 512 * b, 512 * b + n)


def _meet(a, b):
    if a[0] == "ps":
        return a[3] // 512 <= (b[4] - 1) // 512 and b[3] // 512 <= (a[4] - 1) // 512
    if a[2] <= b[1] or b[2] <= a[1] or a[4] <= b[3] or b[4] <= a[3]:
        return False
    if a[5] == 1 and b[5] == 1:
        return True
    return not set(range(a[3], a[4], a[5])).isdisjoint(range(b[3], b[4], b[5]))


def emit(g, T, ops):
    queues = {"pe": g.tensor, "ve": g.vector, "se": g.scalar, "ge": g, "sy": g.sync}
    n = len(ops)
    lane = [o[0] if o[1] == "c" else ("x", i) for i, o in enumerate(ops)]
    known = {q: {} for q in queues}
    clock, waits, wanted = [None] * n, [[] for _ in ops], set()
    by, across = {}, []
    for i, (q, kind, call, rd, wr) in enumerate(ops):
        if kind == "a":
            clock[i] = {lane[i]: i}
        else:
            deps = set()
            for mine, is_w in [(a, False) for a in rd] + [(a, True) for a in wr]:
                for j, other, o_w in by.get(mine[0], []):
                    ps = mine[0] == "ps"
                    if ps and lane[j] == lane[i] and (lane[i] == "pe" or not (is_w or o_w)):
                        continue
                    if (is_w or o_w or ps) and _meet(mine, other):
                        deps.add(j)
            if q == "ve":
                deps.update(across)
                across = [i] if len(set(a[1] // 32 for a in rd)) > 1 else []
            k = known[q]
            for j in sorted(deps, reverse=True):
                if k.get(lane[j], -1) < j:
                    waits[i].append(j)
                    wanted.add(j)
                    for a, b in clock[j].items():
                        if k.get(a, -1) < b:
                            k[a] = b
            clock[i] = dict(k)
            clock[i][lane[i]] = i
        for a in rd:
            by.setdefault(a[0], []).append((i, a, False))
        for a in wr:
            by.setdefault(a[0], []).append((i, a, True))
    mark, count, nd = {}, {q: 0 for q in queues}, 0
    for i, (q, kind, call, rd, wr) in enumerate(ops):
        if kind == "c" and i in wanted:
            count[q] += 1
            mark[i] = (q, count[q])
        elif kind == "a":
            mark[i] = call
        elif kind != "c":
            mark[i] = ("d%d" % nd, call[1])
            nd += 1
    for i, (q, kind, call, rd, wr) in enumerate(ops):
        if kind == "a":
            continue
        for j in waits[i]:
            queues[q].wait_ge(T.sem[mark[j][0]], mark[j][1])
        if kind == "c":
            ins = call(queues[q])
            if i in mark:
                ins.then_inc(T.sem[q], 1)
        else:
            call[0](queues[q], T.sem[mark[i][0]])
    for i, o in enumerate(ops):
        if o[1] != "c" and i not in wanted:
            g.wait_ge(T.sem[mark[i][0]], mark[i][1])


def rank_program(g, core, T, topo):
    r = T.rank_of(core)
    if r is None:
        return
    ALU, ACT = AluOpType, ActivationFunctionType
    ops = []

    def ap(a):
        if isinstance(a, (int, float)) or a is None:
            return a
        if a[0] == "@":
            return ap(a[1]).indirect(ap(a[2]))
        return T[a[0]][a[1]:a[2], a[3]:a[4]:a[5]] if a[5] != 1 else T[a[0]][a[1]:a[2], a[3]:a[4]]

    def regs(*xs):
        out = []
        for a in xs:
            if isinstance(a, tuple):
                out += [a[1], a[2]] if a[0] == "@" else [a]
        return out

    def ind(win, off):
        return ("@", win, off)

    def part(a, p0, p1):
        return (a[0], p0, p1) + a[3:]

    def comp(q, call, rd, wr):
        ops.append([q, "c", call, rd, wr])

    def memset(o, v):
        comp("ve", lambda e: e.memset(ap(o), v), [], [o])

    def copy(o, i):
        if o[0] == "@":
            comp("ve", lambda e: e.tensor_copy(ap(o), ap(i)), [i, o[2]], [o[1]])
        else:
            comp("ve", lambda e: e.tensor_copy(ap(o), ap(i)), regs(i), [o])

    def tt(o, a, b, op):
        comp("ve", lambda e: e.tensor_tensor(ap(o), ap(a), ap(b), op), regs(a, b), [o])

    def ts(o, a, s1, op0, s2=None, op1=None):
        if op1 is None:
            comp("ve", lambda e: e.tensor_scalar(ap(o), ap(a), ap(s1), None, op0), regs(a, s1), [o])
        else:
            comp("ve", lambda e: e.tensor_scalar(ap(o), ap(a), ap(s1), ap(s2), op0, op1), regs(a, s1, s2), [o])

    def scan(o, a, b, init, op0, op1):
        comp("ve", lambda e: e.tensor_tensor_scan(ap(o), ap(a), ap(b), ap(init), op0, op1), regs(a, b, init), [o])

    def least(o, i):
        comp("ve", lambda e: e.tensor_reduce(ap(o), ap(i), AxisListType.X, ALU.min), [i], [o])

    def turn(o, i):
        comp("ve", lambda e: e.transpose(ap(o), ap(i)), [i], [o])

    def quant(qo, so, i):
        comp("ve", lambda e: e.quantize_mx(ap(qo), ap(so), ap(i)), [i], [qo, so])

    def act(o, i, f, bias=0.0, scale=1.0, acc=None):
        if acc is None:
            comp("se", lambda e: e.activation(ap(o), ap(i), f, bias=ap(bias), scale=scale), regs(i, bias), [o])
        else:
            comp("se", lambda e: e.activation(ap(o), ap(i), f, bias=ap(bias), scale=scale, accum_out=ap(acc)), regs(i, bias), [o, acc])

    def actcopy(o, i):
        comp("se", lambda e: e.activation(ap(o), ap(i), ACT.Copy), regs(i), [o])

    def fill(o, v):
        act(o, A("one", 0, len(range(o[3], o[4], o[5])), 1, o[1], o[2]), ACT.Identity, scale=float(v))

    def mm(o, lq, ls, rq, rs):
        comp("pe", lambda e: e.matmul_mx(ap(o), ap(lq), ap(ls), ap(rq), ap(rs), True, True), [lq, ls, rq, rs], [o])

    def unpack(o, b, q, s):
        mm(o, A("eq", 128 * b, 128 * b + 128), A("es", 128 * b, 128 * b + 128), q, s)

    def layer(o, b, q, s):
        mm(o, A("wq", 128 * b, 128 * b + 128), A("wsc", 128 * b, 128 * b + 128), q, s)

    def iota(o, pat, base):
        comp("ge", lambda e: e.iota(ap(o), pat, base, 0, allow_small_or_imprecise_dtypes=True), [], [o])

    def dma(q, out, in_, rd, wr):
        ops.append([q, "d", (lambda e, s: e.dma_start(out, in_).then_inc(s, 16), 16), rd, wr])

    def b8(a):
        return ap(a).bitcast(dt.uint8)

    def dst(k):
        a = topo.addr(T.cores[k])
        return DstId(rid=a[0], pnc=a[1])

    def masks(k, parts):
        e = topo.engines(core, T.cores[k])
        w = len(e) // parts
        return [sum(1 << x for x in e[i * w:(i + 1) * w]) for i in range(parts)], w

    def send_sides(sem, pieces):
        ms, w = masks(pieces[0][0], 2)
        form = lambda a, y: b8(a) if y else ap(a)

        def call(e, s):
            e.remote_dma_fused([RemoteDMATransfer(dst_ids=[dst(k)], dma_engine_mask=ms[0 if k < r else 1], remote_sem=T.sem[sem],
                                                  src=form(a, y), dst=form(b, y)) for k, a, b, y in pieces], local_sem=s)
        ops.append(["ge", "d", (call, w * len(pieces)), [p[1] for p in pieces], []])
        return w

    def arrive(sem, n, wr):
        ops.append(["", "a", (sem, n), [], wr])

    left, right = r > 0, r < N - 1
    sides = int(left) + int(right)
    low_half = r < N // 2
    back_of = lambda k: -(-S * (N // 2 - 1) // (L + 1)) if k < N // 2 else -(-S * (N // 2) // (L + 1))
    back = back_of(r)
    ranks = list(range(0, min(r + 2, N))) if low_half else list(range(r - 1, N))
    nk = len(ranks)
    nr = S * nk
    early = nk >= EARLY
    w0 = 16 + S * ranks.index(r) - back
    k0 = S * r - back
    reach = lambda k: max(0, min(N * S // 2, k + 1, N * S - 1 - k))
    nb = -(-(L * back + reach(k0)) // 16) + 1
    nscan = 5 * (nb + 27)
    ntab = 2 * (16 * nb + L * (NS - back) + reach(k0 + NS - 1))
    z0 = w0 if (r == 0 or not low_half) else 16
    zl = 16 + nr + (0 if right else 16 - back)
    z1 = w0 + NS if low_half else zl + 1
    col = lambda k, at=r: 3 + (k - at) % N
    icol, kcol, m4, quad, quad2 = [A("pk", j, j + 1) for j in range(5)]
    cf = lambda j: A("cf", j, j + 1)
    kc2, mx, vcol, zinit, inic, scol = [cf(j) for j in range(6)]
    off_pair, off_rank, off_spread = A("off", 0, 2), A("off", 2, 6), A("off", 6, 6 + 2 * nk)

    cuts = CUTS
    dma("se", ap(A("ut", 0, 512)), T.u[:], [], [A("ut", 0, 512)])
    for j, (a, b) in enumerate(cuts):
        dma("sy", ap(A("xt", 4 * a, 4 * b)), T.x[:, 4 * a:4 * b], [], [A("xt", 4 * a, 4 * b)])

    def load_w(after):
        dma("sy", b8(A("wq", 0, 512)), T.wc[:], after, [A("wq", 0, 512)])
        dma("sy", ap(A("wsc", 0, 512)), T.ws[:], [], [A("wsc", 0, 512)])
    if not WLATE:
        load_w([A("xt", 0, 4 * C), A("ut", 0, 512)])

    comp("ge", lambda e: e.iota(ap(A("pi", 0, 8)), [[0, 8]], 0, 1), [], [A("pi", 0, 8)])
    memset(A("one", 0, 128), 1.0)
    memset(A("eb", 0, 1040), 0.0)
    comp("ge", lambda e: e.affine_select(ap(A("idn", 0, 128)), ap(A("one", 0, 128)), [[-1, 128]], ALU.is_equal, 0.0, 0, 1),
         [A("one", 0, 128)], [A("idn", 0, 128)])
    iota(A("io16", 0, 112), [[0, 7], [1, 16]], 0)
    iota(A("hf", 0, 16), [[1, 8], [0, 2]], 0)
    iota(A("iof", 0, PW), [[1, PW]], 0)
    io = lambda a, b: A("io16", a, b)
    ts(A("pl", 0, 1), A("pi", 0, 1), 15, ALU.bitwise_and)
    ts(A("pl", 1, 2), A("pi", 0, 1), 31, ALU.bitwise_and)
    ts(A("pl", 2, 3), A("pi", 0, 1), 3, ALU.bitwise_and)
    ts(A("pl", 3, 4), A("pi", 0, 1), 5, ALU.arith_shift_right)
    ts(A("pl", 4, 5), A("pi", 0, 1), 4, ALU.arith_shift_right, 6, ALU.bitwise_and)
    ts(A("pj", 0, 8), A("pi", 0, 8), 7, ALU.bitwise_and)
    copy(A("pk", 0, 5), A("pl", 0, 5))
    ts(A("ms0", 4, 8), A("pj", 4, 8), -1.0, ALU.mult, 7.0, ALU.add)
    ts(A("uoff", 0, 4), A("pj", 0, 4), 16.0, ALU.mult)
    tt(A("ms0", 0, 4), A("ms0", 4, 8), A("pj", 4, 8), ALU.max)
    ts(mx, icol, float(back), ALU.is_ge, PAD, ALU.mult)
    ts(A("rt", 0, 64), io(0, 64), icol, ALU.is_equal, TALL, ALU.mult)
    ts(A("lt16", 0, 16), io(0, 16), icol, ALU.is_lt)
    ts(A("uoff", 4, 8), A("ms0", 0, 4), 16.0, ALU.mult)
    memset(A("d0", 0, nk * BLK), 1.0)
    fill(A("om", EB, EB + 8 * ROW, 3), BIG)
    fill(A("om", EB + 1, EB + 8 * ROW, 3), 0.0)
    for c0 in (2, ROW - 1, ROW - 3):
        fill(A("om", c0, EB + 8 * ROW, ROW), BIG)
    actcopy(A("eb", 2, 514, 4), A("idn", 0, 128))
    actcopy(A("eb", 523, 1035, 4), A("idn", 0, 128))
    quant(A("uq", 0, 128), A("us", 0, 128), A("ut", 0, 512))
    comp("ve", lambda e: e.tensor_copy(ap(A("uq2", 0, 128)).bitcast(dt.uint32), ap(A("uq", 0, 128)).bitcast(dt.uint32).indirect(ap(A("uoff", 0, 8)))),
         [A("uq", 0, 128), A("uoff", 0, 8)], [A("uq2", 0, 128)])
    actcopy(A("us2", 0, 128), ind(A("us", 0, 128), A("uoff", 0, 8)))
    for a, b in cuts:
        quant(A("t0", a, b), A("s0", a, b), A("xt", 4 * a, 4 * b))
    for b in range(4):
        c0 = 520 * (b % 2) + 2 - 2 * (b // 2)
        quant(A("eq", 128 * b, 128 * b + 128), A("es", 128 * b, 128 * b + 128), A("eb", c0, c0 + 512))

    act(A("thc", 16, 112), io(16, 112), ACT.Identity, bias=-1.0)
    act(A("thc", 0, 16), io(0, 16), ACT.Identity, bias=-1.5)
    fill(A("th", 1, 224, 2), -TALL)
    fill(A("th2", 1, 224, 2), -TALL)
    first, ops = ops, []
    act(kc2, kcol, ACT.Identity, bias=2.0 * C * r - 1.0, scale=2.0 * L)
    act(vcol, mx, ACT.Identity, bias=2.0 * (BW - C * r), scale=-1.0)
    act(zinit, mx, ACT.Identity, bias=32.0 * nb - 2 * C * r + 0.5 + (0 if left else 2 * back), scale=-1.0)
    act(scol, A("rt", 15, 16), ACT.Identity, bias=-2.0, scale=2.5 / TALL)
    act(A("ha", 0, NS), A("rt", 16, 64), ACT.Identity, bias=1.0, scale=-1.0 / TALL)
    act(A("hb", 0, NS), A("rt", 15, 63), ACT.Identity, scale=1.25 / TALL)
    act(inic, vcol, ACT.Identity, bias=icol, scale=0.5) if left else act(inic, icol, ACT.Identity, bias=float(BW - 16 * nb - back))
    for j, k in enumerate(ranks):
        a = k // 2
        c0 = BLK * j + 32 * (k % 2)
        act(A("d0", c0, c0 + 32, 1, 32 * a, 32 * a + 32), A("idn", 32 * a, 32 * a + 32, 1, 32 * a, 32 * a + 32), ACT.Identity, bias=1.0, scale=-1.0)
    fill(A("d0", 0, nk * BLK, BLK), 0.0)
    fill(A("d0", BLK - 1, nk * BLK, BLK), -1.0)
    fill(A("eqt", BLK - 1, nk * BLK, BLK, 32, 64), 64.0)
    fill(A("eqt", BLK - 1, nk * BLK, BLK, 64, 128), 64.0)
    fill(A("eqt", BLK - 1, nk * BLK, BLK, 0, 32), 65.0)
    for t in range(R):
        actcopy(A("lp%d" % t, 4, 5), mx)
    fill(A("nst", 0, 4, 1, 64, 128), 0.0)
    fill(A("pf", 0, 16), 0.0)
    fill(A("pf", 48, 96), PAD)
    fill(A("sd", 0, 16), -1.0)
    fill(A("sd", 16 + nr, 16 + nr + 16), -1.0)
    if sides == 1:
        act(cf(12), icol, ACT.Identity, bias=L - 2.0 * L * back + (2 * C * N if left else 0), scale=2.0 * L)
    if not low_half:
        act(A("sd", zl, zl + 1), zinit, ACT.Identity, bias=0.0 if right else 16.0 - back, scale=-0.5)

    def clear(t):
        act(A("win%d" % t, 0, nscan + 5), A("iof", 0, nscan + 5), ACT.Identity, scale=0.0)
        act(A("wim%d" % t, 0, nscan), A("iof", 0, nscan), ACT.Identity, scale=0.0)
        fill(A("win%d" % t, 4, nscan + 5, 5), -16.0)
    later, ops = ops, []
    twice = lambda w: copy(A("tab", w, 2 * w), A("tab", 0, w))
    ts(A("tab", 0, 32, 2), A("lt16", 0, 16), -1.0, ALU.mult)
    tt(A("tab", 1, 32, 2), A("lt16", 0, 16), A("rt", 0, 16), ALU.subtract)
    twice(32)
    ts(A("wi", 0, 4), A("hf", 0, 4), quad2, ALU.add, float(N - r), ALU.add)
    twice(64)
    ts(A("wa", 0, 4), A("wi", 0, 4), N - 1, ALU.bitwise_and)
    twice(128)
    ts(off_pair, io(0, 2), quad2, ALU.add)
    twice(256)
    ts(off_rank, A("wa", 0, 4), 3.0, ALU.add)
    if ALL:
        ts(off_spread, A("hf", 0, 2 * nk), 4.0, ALU.mult, 3.0, ALU.add)
        memset(A("m4", 0, 20), 1.0)
    else:
        copy(off_spread, A("hf", 0, 2 * nk))
    ts(A("d0", 64, nk * BLK, BLK), A("hf", ranks[0], ranks[0] + nk), quad, ALU.is_le)
    for t in range(R):
        memset(A("lc%d" % t, 0, 3), 0.0)
    memset(A("vtl", 4 * NS, 512), 0.0)
    if ALL:
        memset(A("m4", 0, 20, 4), 0.0)
    if sides == 1:
        ts(cf(13), icol, float(back), ALU.is_ge if left else ALU.is_lt)
    spare, ops = ops, []
    tt(A("mk", 0, NS), A("ha", 0, NS), A("hb", 0, NS), ALU.subtract)
    for t in range(R):
        if not left:
            ts(A("lp%d" % t, 0, 1), cf(12), cf(13), ALU.mult, mx, ALU.add)
        if not right:
            ts(A("lp%d" % t, 8, 9), cf(12), cf(13), ALU.mult)
    last, ops = ops, first

    def gap(cnt=1):
        ops.extend(spare[:cnt])
        del spare[:cnt]

    for t in range(R):
        n = lambda s: s + str(t)
        tq, tsc, fh = n("t"), n("s"), n("fh")
        pc, psc = [], []
        if left:
            pc.append((r - 1, A(tq, 0, BW), A(n("lt"), BW, 2 * BW), True))
            psc.append((r - 1, A(tsc, 0, BW), A(n("ls"), BW, 2 * BW), False))
        if right:
            pc.append((r + 1, A(tq, C - BW, C), A(n("lt"), 0, BW), True))
            psc.append((r + 1, A(tsc, C - BW, C), A(n("ls"), 0, BW), False))
        w = send_sides(n("at"), pc)
        send_sides(n("at"), psc)
        l0, l1 = (0 if left else BW), (2 * BW if right else BW)
        arrive(n("at"), 2 * w * sides, [A(n("lt"), l0, l1), A(n("ls"), l0, l1)])
        cut = PIECES[-1][0] if t else cuts[-1][0]
        for h, (c0, c1) in enumerate([(0, cut), (cut, C)]):
            mm(bank(4 + h, c1 - c0), A("uq2", 0, 128), A("us2", 0, 128), A(tq, c0, c1), A(tsc, c0, c1))
            act(A("ys", c0, c1), bank(4 + h, c1 - c0), ACT.Abs)
        for b in range(4):
            unpack(bank(b, C), b, A(tq, 0, C), A(tsc, 0, C))
        if t == R - 1:
            quant(A("vq", 0, 128), A("vs", 0, 128), A("vt", 0, 512))
        else:
            gap(2)
        for l in range(L):
            turn(A("om", EB + 3 * l + 5, EB + 32 * ROW, ROW), A("ys", l, C, L))
        fown = lambda b: actcopy(A(fh, PW * b + BW, PW * b + BW + C), bank(b, C))
        om = lambda a, cnt, st=3: A("om", a, a + st * (cnt - 1) + 1, st)
        o_ = lambda k: EB - ROW * k
        pair = lambda k: tt(om(o_(k) + 7, 15), om(o_(k) + 2, 15), om(o_(k) + 5, 15), ALU.min)

        def step(k, p0=0, p1=128, q0=None):
            q0 = p0 if q0 is None else q0
            scan(part(om(o_(k) + 3, 42, 1), p0, p1), part(om(o_(k - 1) + 6, 42, 1), q0, q0 + p1 - p0), part(om(EB + ROW * k + 3, 42, 1), p0, p1),
                 0.0, ALU.min, ALU.max)
        for b in range(4):
            fown(b)
        if t == 0:
            ops.extend(later)
        gap(2)
        for k in range(1, 4):
            pair(k - 1)
            gap(2)
            step(k)
            gap(2)
        pair(3)
        gap(2)
        if t == 0:
            for c0 in range(512, ntab, 512):
                actcopy(A("tab", c0, min(ntab, c0 + 512)), A("tab", 0, min(ntab - c0, 512)))
        lo3 = om(o_(3) + 10, 13)
        cost = A(n("lc"), 3, 4)
        step(4)
        tt(A("cm", 0, 13, 1, 0, 64), part(lo3, 0, 64), part(lo3, 64, 128), ALU.max)
        least(part(cost, 0, 64), A("cm", 0, 13, 1, 0, 64))
        least(part(cost, 64, 128), A("cm", 0, 13, 1, 0, 64))
        others = sorted(set(range(N)) - {r}, key=lambda k: (abs(2 * k - N + 1), (k - r) % N)) if ORDER else [(r + d) % N for d in range(1, N)]
        full, wf = masks(others[0], 1)

        def send_costs(e, s, t=t, cost=cost, full=full, others=others):
            e.remote_dma_fused([RemoteDMATransfer(dst_ids=[dst(k) for k in others], dma_engine_mask=full[0], remote_sem=T.sem["ac%d" % t],
                                                  srcs=[ap(cost)], dsts=[ap(A("lc%d" % t, col(r, k), col(r, k) + 1)) for k in others])], local_sem=s)
        ops.append(["ge", "d", (send_costs, wf), [cost], []])
        arrive("ac%d" % t, wf * (N - 1), [A(n("lc"), 4, 3 + N)])

        def borrowed(b, move):
            unpack(bank(b, l1 - l0), b, A(n("lt"), l0, l1), A(n("ls"), l0, l1))
            if left:
                move(A(fh, PW * b, PW * b + BW), bank(b, BW))
            if right:
                c0 = 512 * b + (BW if left else 0)
                move(A(fh, PW * b + BW + C, PW * b + FW), A("ps", c0, c0 + BW))
            if sides == 1:
                c0 = PW * b + (BW + C if left else 0)
                fill(A(fh, c0, c0 + BW), 0.0)
        o6 = o_(6)
        tx = lambda a, b: tt(A("tx", a, b), om(o6 + 3 * a + 2, b - a), om(o6 + 3 * a + 10, b - a), ALU.is_le)
        ty = lambda a, b: tt(A("ty", a, b), om(o6 + 3 * a + 4, b - a), om(o6 + 3 * a + 5, b - a), ALU.is_le)
        tz = lambda a, b: tt(A("tz", a, b), A("tx", a, b), A("thc", a, b), ALU.add)
        even = lambda name, a, b: A(name, 2 * a, 2 * b - 1, 2)
        th = lambda a, b: tt(even("th", a, b), A("tz", a, b), A("ty", a, b), ALU.add)
        u1 = lambda a, b: tt(A("u1", a, b), A("ty", a, b), even("th", a - 16, b - 16), ALU.mult)
        u2 = lambda a, b: tt(A("u2", a, b), A("tx", a, b), even("th", a - 15, b - 15), ALU.mult)
        u3 = lambda a, b: tt(A("u3", a, b), A("u1", a, b), A("u2", a, b), ALU.max)
        th2 = lambda a, b: tt(even("th2", a, b), A("u3", a, b), even("th", a - 17, b - 17), ALU.max)
        spread = lambda: copy(A("bc", 0, 64), ind(A(n("lc"), 0, 3 + N), off_rank))
        pair(4)
        tx(48, 111)
        ty(48, 111)
        step(5)
        tz(48, 111)
        pair(5)
        th(48, 111)
        step(6)
        tx(16, 47)
        ty(16, 47)
        pair(6)
        tz(16, 47)
        u1(65, 110)
        u2(65, 110)
        step(7)
        tx(1, 14)
        th(16, 47)
        ty(1, 14)
        scan(A("pc", 0, L), om(5, L), om(5, L), BIG, ALU.min, ALU.min)
        tz(1, 14)
        u1(33, 46)
        u2(33, 46)
        u3(65, 110)
        th(1, 14)
        u3(33, 46)
        th2(65, 110)
        gap(len(spare))
        if FIRST:
            spread()
        th2(33, 46)
        if not FIRST:
            spread()
        nst = lambda k, k1=None: A("nst", k, k1 or k + 1, 1, 0, 64)
        act(A("junk2", 0, L, 1, 0, 64), A("pc", 0, L, 1, 0, 64), ACT.Sign, bias=part(cost, 0, 64), scale=-1.0, acc=nst(8))

        def back_to(k, frm, name):
            o = 32 * (6 - k) + 1
            act(A("junk2", 32 * k + 32, 32 * k + 59, 1, 0, 64), A(name, o, o + 27, 1, 0, 64), ACT.Sign, bias=nst(frm),
                scale=1.0 if frm == 8 else 2.0, acc=nst(k))
        lc = lambda k: A(n("lc"), col(k), col(k) + 1)
        if WLATE and t == 0:
            load_w([nst(8)])
        back_to(6, 8, "th")
        act(nst(7), nst(8), ACT.Identity, bias=-1.0, scale=2.0)
        back_to(4, 6, "th2")
        back_to(5, 6, "th")
        back_to(2, 4, "th2")
        back_to(3, 4, "th")
        actcopy(part(nst(4, 8), 64, 128), nst(4, 8))
        back_to(0, 2, "th2")
        back_to(1, 2, "th")
        act(A("bn", 0, 32), ind(A("nst", 0, 8), off_pair), ACT.Identity, bias=kc2, scale=-1.0)
        for b in range(BOR):
            borrowed(b, actcopy)
        turn(A("aa", 0, 64), A("bc", 0, 64))
        if t == 0:
            ops.extend(last)
        for j, k in enumerate(ranks):
            ts(A("eqt", BLK * j, BLK * j + 64), A("aa", 0, 64), lc(k), ALU.is_equal, 2.0, ALU.mult)
            ts(A("eqt", BLK * j + 64, BLK * j + 128), A("aa", 0, 64), lc(k), ALU.is_gt, 2.0, ALU.mult)
        ends = A("sct", BLK - 1, nk * BLK, BLK)

        def flags():
            j = (nk + 1) // 2 if SPLIT else nk
            cc = A("cc4", 0, 4 * nk) if ALL else A("cc", 0, nk)
            ts(A("bfl", 0, S * j), ind(cc, A("off", 6, 6 + 2 * j)), -1.0, ALU.max, 1.0, ALU.min)
            if j < nk:
                act(A("bfl", S * j, nr), ind(cc, A("off", 6 + 2 * j, 6 + 2 * nk)), ACT.Sign)
        count = [lambda: scan(A("sct", 0, nk * BLK), A("d0", 0, nk * BLK), A("eqt", 0, nk * BLK), 0.0, ALU.mult, ALU.add),
                 lambda: tt(A("hh", 0, nk, 1, 0, 64), part(ends, 0, 64), part(ends, 64, 128), ALU.add),
                 lambda: tt(A("cc", 0, nk, 1, 0, 32), A("hh", 0, nk, 1, 0, 32), A("hh", 0, nk, 1, 32, 64), ALU.add),
                 lambda: [(copy if q < 3 or not SPLIT else actcopy)(A("cc", 0, nk, 1, 32 * q, 32 * q + 32), A("cc", 0, nk, 1, 0, 32)) for q in range(1, 4)],
                 flags,
                 lambda: turn(A("sd", 16, 16 + nr), A("bfl", 0, nr))]
        if ALL:
            def share():
                moves = [(0, 128, 0, 0), (0, 64, 64, 1), (64, 128, 0, 1)] + [(32 * q, 32 * q + 32, 32 * (q ^ x), 1 + (x + 1) // 2) for x in (1, 3) for q in range(4)]
                for i, (p0, p1, q0, slot) in enumerate(moves):
                    (actcopy if i % 2 else copy)(A("hh", slot, 4 * nk, 4, q0, q0 + p1 - p0), part(ends, p0, p1))
            count[1:4] = [share, lambda: scan(A("cc4", 0, 4 * nk), A("m4", 0, 4 * nk), A("hh", 0, 4 * nk), 0.0, ALU.mult, ALU.add)]
        for f in count[:AT]:
            f()
        turn(A("pf", 16, 48), A("bn", 0, 32))
        for f in count[AT:AT2]:
            f()
        wps = n("wps")
        pick = lambda o, c0, cnt: scan(A(wps, o, o + cnt), A("rt", 0, cnt), A("pf", c0, c0 + cnt), 0.0, ALU.add, ALU.min)
        to_left, to_right = A(wps, 15, 16), A(wps, 47, 48)
        if left and back_of(r - 1) != back:
            pick(48, 16 - back_of(r - 1), 16)
            to_left = A(wps, 63, 64)
        if right and back_of(r + 1) != back:
            pick(48, 48 - back_of(r + 1), 16)
            to_right = A(wps, 63, 64)
        pick(0, 16 - back, NS)
        pp = []
        if left:
            pp.append((r - 1, to_left, A(n("lp"), 8, 9), False))
        if right:
            pp.append((r + 1, to_right, A(n("lp"), 0, 1), False))
        w = send_sides(n("ap"), pp)
        arrive(n("ap"), w * sides, ([A(n("lp"), 0, 1)] if left else []) + ([A(n("lp"), 8, 9)] if right else []))
        if t == 0:
            dma("sy", ap(A("vt", 0, 512)), T.v[:], [A("lp0", 0, 9)], [A("vt", 0, 512)])
        for f in count[AT2:]:
            f()
            if f == count[1]:
                for b in range(BOR, BOR2):
                    borrowed(b, actcopy)
        for b in range(BOR2, 4):
            borrowed(b, actcopy)
        clear(t)
        own, voff, sdw = A(wps, 15, 48, 16), A(n("voff"), 0, 3), A("sd", w0, w0 + NS)
        land = lambda j: A(n("lp"), 4 * j, 4 * j + 1)
        to_v = lambda j: ts(A(n("voff"), j, j + 1), A("wp", j, j + 1), land(j), ALU.add, 0.5, ALU.mult)
        to_e = lambda j: ts(A("eo", j, j + 1), A("ta", j, j + 1), A("tb", j, j + 1), ALU.add, land(j), ALU.add)
        gv = lambda move, b: move(A("vtl", b, 4 * NS, 4), ind(A(fh, PW * b, PW * b + FW), voff))
        ha = lambda: tt(A("ha", 0, NS), ind(A("iof", 0, FW - 1), voff), A("iof", FW - 1, PW - 1), ALU.subtract)
        ts(A("wp", 0, 3), own, vcol, ALU.add)
        scan(A("zs", z0, z1), A("sd", z0, z1), A("sd", z0, z1), zinit if low_half else 0.0, ALU.add, ALU.add)
        scan(A("rr", 0, NS), A("mk", 0, NS), sdw, 0.0, ALU.mult, ALU.add)
        to_v(1)
        if WP == 0:
            to_v(0)
            to_v(2)
        tt(A("tb", 0, 3), A("zs", w0 + 15, w0 + NS, 16), own, ALU.add)
        if low_half:
            ts(A("ta", 0, 3), A("rr", 15, NS, 16), scol, ALU.mult)
        else:
            ts(A("ta", 0, 3), A("rr", 15, NS, 16), scol, ALU.mult, A("zs", zl, zl + 1), ALU.subtract)
        if left:
            act(A("ini", 0, 1), A("zs", w0 - 1, w0) if low_half else A("zs", zl, zl + 1), ACT.Identity, bias=inic, scale=-0.5 if low_half else 0.5)
        ini = A("ini", 0, 1) if left else inic
        if WP == 1:
            to_v(0)
            to_v(2)
        if WP == 0:
            ha()
        for b in range(VV, 4):
            gv(actcopy, b)
        for j in (1, 0, 2):
            to_e(j)
        if WP == 1:
            ha()
        for b in range(VV):
            gv(copy, b)
        ts(A("wa", 0, 3), A("eo", 0, 3), 1.0 / 32, ALU.mult, -31.0 / 64, ALU.add)
        tt(A("vv1", 0, NS), ind(A("tab", 0, ntab), A("eo", 0, 3)), A("ha", 0, NS), ALU.max)
        if QV == 0:
            quant(A(n("qv"), 0, 128), A(n("sv"), 0, 128), A("vtl", 0, 512))
        ts(A("so", 0, 3), A("wa", 0, 3), 5.0, ALU.mult, m4, ALU.add)
        if QV == 1:
            quant(A(n("qv"), 0, 128), A(n("sv"), 0, 128), A("vtl", 0, 512))
        if t == R - 1:
            act(A("junk2", 256, 288), A("pf", 16, 48), ACT.Identity, bias=-float(C * r), scale=0.5)
            dma("sy", T.ol[:], T["junk2"][0:128:16, 256:288], [A("junk2", 256, 288)], [])
        tt(A("vv2", 0, NS), A("vv1", 0, NS), sdw, ALU.subtract)
        for b in range(4):
            layer(bank(b, 128), b, A(n("qv"), 0, 128), A(n("sv"), 0, 128))
            act(A(fh, PW * b + FW, PW * b + PW), bank(b, NS), ACT.Relu, scale=0.03125)
        copy(ind(A(n("win"), 0, 320), A("so", 0, 3)), A("vv1", 0, NS))
        copy(ind(A(n("wim"), 0, 320), A("so", 0, 3)), A("vv2", 0, NS))
        m0 = PIECES[0][1] // 16 if HALVES else 28
        n0 = 5 * (nb + m0 - 1)
        scan(A("sc", 0, n0), A(n("wim"), 0, n0), A(n("win"), 5, n0 + 5), ini, ALU.add, ALU.subtract)
        copy(A(n("eoff"), 0, m0), A("sc", 5 * nb - 1, n0, 5))
        if HALVES:
            scan(A("sc", n0, nscan), A(n("wim"), n0, nscan), A(n("win"), n0 + 5, nscan + 5), A("sc", n0 - 1, n0), ALU.add, ALU.subtract)
        rest = lambda h, b: copy(A(n("eoff"), m0, 28), A("sc", n0 + 4, nscan, 5)) if HALVES else None
        nq, nsc = "t%d" % (t + 1), "s%d" % (t + 1)
        etl, xn = n("etl"), n("xn")
        cols = lambda name, h: A(name, *PIECES[h])
        wide = lambda h: PIECES[h][1] - PIECES[h][0]
        tile = lambda name, h: A(name, 4 * PIECES[h][0], 4 * PIECES[h][1])
        plane = lambda name, h, b: A(name, 4 * PIECES[h][0] + b, 4 * PIECES[h][1], 4)
        gather = lambda move, h, b: move(plane(etl, h, b), ind(A(fh, PW * b, PW * b + PW), A(n("eoff"), PIECES[h][0] // 16, PIECES[h][1] // 16)))
        qe = lambda h: quant(cols(n("qe"), h), cols(n("se"), h), tile(etl, h))
        qx = lambda h: quant(cols(nq, h), cols(nsc, h), tile(xn, h))
        rl = lambda h, b: A("rl", C * b + PIECES[h][0], C * b + PIECES[h][1])
        relu = lambda h, b: act(rl(h, b), bank(4 + b, wide(h)), ACT.Relu, scale=0.015625)
        add = lambda h, b: tt(plane(xn, h, b), bank(b, wide(h)), rl(h, b), ALU.add)

        def products(h, b):
            layer(bank(4 + b, wide(h)), b, cols(n("qe"), h), cols(n("se"), h))
            unpack(bank(b, wide(h)), b, cols(n("qe"), h), cols(n("se"), h))
        vrelu = lambda h, b: ts(rl(h, b), bank(4 + b, wide(h)), 0.0, ALU.max, 0.015625, ALU.mult)
        calls = {"g": lambda h, b: gather(copy, h, b), "G": lambda h, b: gather(actcopy, h, b), "e": lambda h, b: qe(h), "x": lambda h, b: qx(h),
                 "p": products, "R": relu, "r": vrelu, "a": add, "o": rest,
                 "w": lambda h, b: layer(bank(4 + b, wide(h)), b, cols(n("qe"), h), cols(n("se"), h)),
                 "u": lambda h, b: unpack(bank(b, wide(h)), b, cols(n("qe"), h), cols(n("se"), h))}
        for word in TAIL.split():
            calls[word[0]](int(word[1]), int(word[2:] or 0))

    for h, (c0, c1) in enumerate([(0, PIECES[-1][0]), PIECES[-1]]):
        dma("sy", T.oc[:, 4 * c0:4 * c1], b8(A("t2", c0, c1)), [A("t2", c0, c1)], [])
        mm(bank(4 + h, c1 - c0), A("vq", 0, 128), A("vs", 0, 128), A("t2", c0, c1), A("s2", c0, c1))
        actcopy(A("ys", c0, c1), bank(4 + h, c1 - c0))
        dma("se", T.y[:, c0:c1], ap(A("ys", c0, c1)), [A("ys", c0, c1)], [])
    for k in range(4):
        dma("sy", T.osc[4 * k:4 * k + 4, 0:C], T.s2[32 * k:32 * k + 4, 0:C], [A("s2", 0, C)], [])
    emit(g, T, ops)
